import numpy as np
import ml_dtypes


def mxq(x, axis, fmt="e4m3"):
    dtype, down = {"e4m3": (ml_dtypes.float8_e4m3fn, 7), "e5m2": (ml_dtypes.float8_e5m2, 14)}[fmt]
    v = np.moveaxis(np.asarray(x, np.float32).astype(ml_dtypes.bfloat16).astype(np.float64), axis, -1)
    blocks = v.reshape(v.shape[:-1] + (-1, 32))
    amax = np.abs(blocks).max(-1, keepdims=True)
    byte = np.maximum(np.where(amax > 0, np.frexp(amax)[1] - 1 + 127, 0) - down, 1)
    scale = np.exp2(byte - 127.0)
    codes = (blocks / scale).astype(np.float32).astype(dtype).astype(np.float64)
    return np.moveaxis((codes * scale).reshape(v.shape), -1, axis)


WIDE = False


def mx_kscale(k):
    if not WIDE:
        return np.ones(k)
    levels = np.array([30, -30])
    if k % 512:
        return np.exp2(np.random.permutation(np.resize(levels, k // 32))).repeat(32)
    a = np.empty((k // 512, 16))
    for p in range(k // 512):
        a[p, :8] = np.random.permutation(np.resize(levels, 8))
        for g in range(8):
            far = levels[np.abs(levels - a[p, g]) >= 10]
            a[p, g + 8] = far[np.random.randint(len(far))]
    return np.exp2(a.ravel()).repeat(32)


def f64(x):
    return np.asarray(x).astype(np.float64)


K, N, T = 1024, 512, 1024


def setup_inputs():
    n = np.random.standard_normal
    s = mx_kscale(K)[:, None]
    return {
        "w": (n((K, N)) / np.sqrt(K) / s).astype(np.float32),
        "x": (n((K, T)) * s).astype(np.float32),
        "res": (n((N, T))).astype(np.float32),
    }


def reference(w, x, res):
    w_q_ = mxq(f64(w), 0, "e4m3")
    w_r_ = mxq(f64(w) - w_q_, 0, "e5m2")
    x_q_ = mxq(f64(x), 0, "e4m3")
    x_r_ = mxq(f64(x) - x_q_, 0, "e5m2")
    y = w_q_.T @ x_q_ + w_q_.T @ x_r_ + w_r_.T @ x_q_ + w_r_.T @ x_r_
    return f64(res) + y

@@ -1,0 +1,243 @@
+from contextlib import ExitStack
+
+import concourse.mybir as mybir
+from concourse.masks import make_identity
+
+K, N, T = 1024, 512, 1024
+FLOPS = 4 * 2 * K * N * T
+
+F32 = mybir.dt.float32
+BF16 = mybir.dt.bfloat16
+U32 = mybir.dt.uint32
+U8 = mybir.dt.uint8
+FMT = {"q": mybir.dt.float8_e4m3fn_x4, "r": mybir.dt.float8_e5m2_x4}
+
+P = 128
+PACK = 4
+K_PASS = P * PACK
+WIDE = 512
+CH = 128
+PER = WIDE // CH
+UNITS = [("x", 0, 0), ("w", 0, 0), ("x", 1, 0), ("w", 1, 0), ("x", 0, 1), ("x", 1, 1)]
+NCH = PER * len(UNITS)
+LOADS = [[2, 2], [2, 2], [4], [4], [4], [4]]
+QW = (1, 1, 2, 4, 4, 4)
+RW = (4, 1, 4, 1, 4, 4)
+QSTEP = [-2, -1, 0, 1, 2, 3, 4, 5, 6, 6, 8, 8, 10, 10, 10, 10, 13, 13, 13, 13, 17, 17, 17, 17]
+LD = 2
+BUD = 3
+BUDF = 4
+FL = 2
+LAG = 1
+RUN_CAST = 4
+RUN_SUB = 4
+VCAST = (0,)
+WARM = 0
+RES_AFTER = (4, 5)
+LAST_SPLIT = 2
+
+
+def tile_mix_tierb_four_res_kernel(tc, w, x, res, out):
+    nc = tc.nc
+    with ExitStack() as ctx:
+        sb = ctx.enter_context(tc.tile_pool(name="sb", bufs=1))
+        ps = ctx.enter_context(tc.psum_pool(name="ps", bufs=1))
+        ctx.enter_context(tc.manual_schedule())
+
+        raw = {}
+        res_sb = {}
+
+        def load_res(h):
+            res_sb[h] = sb.tile([P, PER, WIDE], F32, name="res%d" % h)
+            nc.sync.dma_start(
+                out=res_sb[h][:],
+                in_=res[:, h * WIDE : (h + 1) * WIDE].rearrange("(i p) t -> p i t", p=P),
+            )
+
+        for u, (kind, g, h) in enumerate(UNITS):
+            src = x if kind == "x" else w
+            c = 0
+            for n in LOADS[u]:
+                piece = sb.tile([P, PACK, n * CH], F32, name="raw%d_%d" % (u, c), align_bytes=64)
+                col = h * WIDE + c * CH
+                nc.sync.dma_start(
+                    out=piece[:],
+                    in_=src[g * K_PASS : (g + 1) * K_PASS, col : col + n * CH].rearrange(
+                        "(p j) c -> p j c", j=PACK
+                    ),
+                )
+                for i in range(n):
+                    raw[PER * u + c + i] = (piece, i * CH)
+                c = c + n
+            for hh in range(2):
+                if RES_AFTER[hh] == u:
+                    load_res(hh)
+
+        eye = sb.tile([P, P], BF16, name="eye", align_bytes=64)
+        make_identity(nc, eye[:])
+        spread = sb.tile([P, PACK * (K_PASS + 1)], BF16, name="spread", align_bytes=64)
+        nc.vector.memset(spread[:].bitcast(U32), 0)
+        nc.vector.tensor_copy(
+            out=spread[:].rearrange("p (j r) -> p j r", j=PACK)[:, :, 0:K_PASS:PACK],
+            in_=eye[:].unsqueeze(1).to_broadcast([P, PACK, P]),
+        )
+        eye_codes = sb.tile([P, K_PASS], U32, name="eye_codes", align_bytes=256)
+        eye_scales = sb.tile([P, K_PASS], U8, name="eye_scales", align_bytes=256)
+        nc.vector.quantize_mx(
+            out=eye_codes[:].bitcast(FMT["q"]), scales=eye_scales[:], in_=spread[:, 0 : PACK * K_PASS]
+        )
+        if WARM:
+            warm = ps.tile([P, WIDE], F32, name="warm", tag="acc0")
+            for i in range(WARM):
+                nc.tensor.matmul_mx(
+                    out=warm[:], lhsT=eye_codes[:, 0:P].bitcast(FMT["q"]), lhsT_scale=eye_scales[:, 0:P],
+                    rhs=eye_codes[:].bitcast(FMT["q"]), rhs_scale=eye_scales[:], start=True, stop=True,
+                )
+
+        bf = {}
+        codes = {}
+        scales = {}
+        for u in range(len(UNITS)):
+            for tier in "qr":
+                bf[tier, u] = sb.tile([P, WIDE * PACK], BF16, name="bf_%s%d" % (tier, u), align_bytes=256)
+                codes[tier, u] = sb.tile([P, WIDE], U32, name="codes_%s%d" % (tier, u), align_bytes=256)
+                scales[tier, u] = sb.tile([P, WIDE], U8, name="scales_%s%d" % (tier, u), align_bytes=256)
+
+        def grouped(tier, c0, n, run):
+            lo = (c0 % PER) * CH * PACK
+            return bf[tier, c0 // PER][:, lo : lo + n * CH * PACK].rearrange("p (c i j) -> p c j i", i=run, j=PACK)
+
+        def rows(c0, n, run):
+            piece, lo = raw[c0]
+            return piece[:, :, lo : lo + n * CH].rearrange("p j (c i) -> p c j i", i=run)
+
+        def cast(c0, n):
+            c = c0
+            while c < c0 + n:
+                m = 1
+                while c + m < c0 + n and raw[c + m][0] is raw[c][0]:
+                    m = m + 1
+                if c in VCAST:
+                    nc.vector.tensor_copy(out=grouped("q", c, m, RUN_CAST), in_=rows(c, m, RUN_CAST))
+                else:
+                    nc.scalar.copy(out=grouped("q", c, m, RUN_CAST), in_=rows(c, m, RUN_CAST))
+                c = c + m
+
+        def quant(tier, c0, n):
+            u, lo = c0 // PER, (c0 % PER) * CH
+            nc.vector.quantize_mx(
+                out=codes[tier, u][:, lo : lo + n * CH].bitcast(FMT[tier]),
+                scales=scales[tier, u][:, lo : lo + n * CH],
+                in_=bf[tier, u][:, lo * PACK : (lo + n * CH) * PACK],
+            )
+
+        back = {}
+
+        def dequant(c):
+            u, lo = c // PER, (c % PER) * CH
+            back[c] = ps.tile([P, PACK, CH], F32, name="back%d" % c, tag="back%d" % (c % 4))
+            for j in range(PACK):
+                nc.tensor.matmul_mx(
+                    out=back[c][:, j, :],
+                    lhsT=eye_codes[:, j * P : (j + 1) * P].bitcast(FMT["q"]),
+                    lhsT_scale=eye_scales[:, j * P : (j + 1) * P],
+                    rhs=codes["q", u][:, lo : lo + CH].bitcast(FMT["q"]),
+                    rhs_scale=scales["q", u][:, lo : lo + CH],
+                    start=True,
+                    stop=True,
+                )
+
+        def sub(c):
+            nc.vector.tensor_tensor(
+                out=grouped("r", c, 1, RUN_SUB),
+                in0=rows(c, 1, RUN_SUB),
+                in1=back[c][:].rearrange("p j (c i) -> p c j i", i=RUN_SUB),
+                op=mybir.AluOpType.subtract,
+            )
+
+        acc = {}
+
+        def product(p, start, stop):
+            h, g, t, wt, xt = p
+            xu, wu = UNITS.index(("x", g, h)), UNITS.index(("w", g, 0))
+            if start:
+                acc[h, t] = ps.tile([P, WIDE], F32, name="acc%d_%d" % (h, t), tag="acc%d" % t)
+            nc.tensor.matmul_mx(
+                out=acc[h, t][:],
+                lhsT=codes[wt, wu][:, t * P : (t + 1) * P].bitcast(FMT[wt]),
+                lhsT_scale=scales[wt, wu][:, t * P : (t + 1) * P],
+                rhs=codes[xt, xu][:].bitcast(FMT[xt]),
+                rhs_scale=scales[xt, xu][:],
+                start=start,
+                stop=stop,
+            )
+
+        def finish(key):
+            h, t = key
+            parts = LAST_SPLIT if key == (1, PER - 1) else 1
+            width = WIDE // parts
+            for i in range(parts):
+                cols = slice(i * width, (i + 1) * width)
+                o = sb.tile([P, width], F32, name="o%d_%d_%d" % (h, t, i))
+                nc.vector.tensor_tensor(out=o[:], in0=res_sb[h][:, t, cols], in1=acc[h, t][:, cols], op=mybir.AluOpType.add)
+                eng = nc.scalar if (parts > 1 and i % 2 == 1) else nc.sync
+                eng.dma_start(out=out[t * P : (t + 1) * P, h * WIDE + i * width : h * WIDE + (i + 1) * width], in_=o[:])
+
+        ready = {}
+        count = {}
+        todo = [(h, g, t, wt, xt) for h in range(2) for g in range(2) for t in range(PER) for xt in "qr" for wt in "qr"]
+        finished = set()
+        closing = []
+
+        def can_run(p, step):
+            h, g, t, wt, xt = p
+            if h == 1 and (0, t) not in finished:
+                return False
+            xu, wu = UNITS.index(("x", g, h)), UNITS.index(("w", g, 0))
+            return ready.get((wt, PER * wu + t), 99) <= step and all(
+                ready.get((xt, PER * xu + i), 99) <= step for i in range(PER)
+            )
+
+        def products(n, ready_by, stamp):
+            for i in range(n):
+                cands = [p for p in todo if can_run(p, ready_by)]
+                if not cands:
+                    return
+                p = cands[0]
+                todo.remove(p)
+                key = (p[0], p[2])
+                count[key] = count.get(key, 0) + 1
+                product(p, count[key] == 1, count[key] == 8)
+                if count[key] == 8:
+                    closing.append((stamp, key))
+
+        for step in range(-6, NCH + 20):
+            for c0 in range(NCH):
+                n = QW[c0 // PER]
+                if c0 % n == 0 and QSTEP[c0] == step:
+                    cast(c0, n)
+                    quant("q", c0, n)
+                    for i in range(n):
+                        ready["q", c0 + i] = step
+            for c in range(NCH):
+                if max(QSTEP[c - c % QW[c // PER]], c - LD) == step:
+                    dequant(c)
+            if 0 <= step < NCH:
+                sub(step)
+            fin = [k for s, k in closing if s + FL <= step and k not in finished][: 1 if step < NCH else PER]
+            c = step - 1
+            if 0 <= c < NCH and (c + 1) % RW[c // PER] == 0:
+                n = RW[c // PER]
+                quant("r", c + 1 - n, n)
+                for i in range(n):
+                    ready["r", c + 1 - n + i] = step
+            for k in fin:
+                finish(k)
+            if step >= NCH:
+                todo = sorted(todo, key=lambda p: (p[0], p[2]))
+                products(2, step, step - FL + 1)
+            else:
+                products(BUDF if fin else BUD, step - LAG, step)
+            for k in fin:
+                finished.add(k)
+        assert not todo and len(finished) == 8

@@ -1,7 +1,6 @@
 from contextlib import ExitStack
 
 import concourse.mybir as mybir
-from concourse.masks import make_identity
 
 K, N, T = 1024, 512, 1024
 FLOPS = 4 * 2 * K * N * T
@@ -10,31 +9,28 @@ F32 = mybir.dt.float32
 BF16 = mybir.dt.bfloat16
 U32 = mybir.dt.uint32
 U8 = mybir.dt.uint8
-FMT = {"q": mybir.dt.float8_e4m3fn_x4, "r": mybir.dt.float8_e5m2_x4}
+FORMAT = {"q": mybir.dt.float8_e4m3fn_x4, "r": mybir.dt.float8_e5m2_x4}
 
 P = 128
 PACK = 4
 K_PASS = P * PACK
 WIDE = 512
-CH = 128
-PER = WIDE // CH
-UNITS = [("x", 0, 0), ("w", 0, 0), ("x", 1, 0), ("w", 1, 0), ("x", 0, 1), ("x", 1, 1)]
-NCH = PER * len(UNITS)
-LOADS = [[2, 2], [2, 2], [4], [4], [4], [4]]
-QW = (1, 1, 2, 4, 4, 4)
-RW = (4, 1, 4, 1, 4, 4)
-QSTEP = [-2, -1, 0, 1, 2, 3, 4, 5, 6, 6, 8, 8, 10, 10, 10, 10, 13, 13, 13, 13, 17, 17, 17, 17]
-LD = 2
-BUD = 3
-BUDF = 4
-FL = 2
-LAG = 1
-RUN_CAST = 4
-RUN_SUB = 4
-VCAST = (0,)
-WARM = 0
-RES_AFTER = (4, 5)
-LAST_SPLIT = 2
+CHUNK = 128
+PER_SLAB = WIDE // CHUNK
+HALF = PER_SLAB // 2
+SLABS = [("x", 0, 0), ("w", 0, 0), ("x", 1, 0), ("w", 1, 0), ("x", 0, 1), ("x", 1, 1)]
+CHUNKS = PER_SLAB * len(SLABS)
+PASSES_PER_TILE = 4 * (K // K_PASS)
+BACK_BANKS = 4
+RUN = 2
+HALVED_LOADS = 3
+MAX_LEAD = 3
+BACK_LEAD = 2
+PRODUCTS_PER_STEP = 3
+DRAIN_DELAY = 2
+WARM_HEAD = 0
+WARM_EACH = 0
+WARM_UNTIL = 0
 
 
 def tile_mix_tierb_four_res_kernel(tc, w, x, res, out):
@@ -45,199 +41,194 @@ def tile_mix_tierb_four_res_kernel(tc, w, x, res, out):
         ctx.enter_context(tc.manual_schedule())
 
         raw = {}
-        res_sb = {}
-
-        def load_res(h):
-            res_sb[h] = sb.tile([P, PER, WIDE], F32, name="res%d" % h)
-            nc.sync.dma_start(
-                out=res_sb[h][:],
-                in_=res[:, h * WIDE : (h + 1) * WIDE].rearrange("(i p) t -> p i t", p=P),
-            )
-
-        for u, (kind, g, h) in enumerate(UNITS):
+        for s, (kind, g, h) in enumerate(SLABS):
             src = x if kind == "x" else w
-            c = 0
-            for n in LOADS[u]:
-                piece = sb.tile([P, PACK, n * CH], F32, name="raw%d_%d" % (u, c), align_bytes=64)
-                col = h * WIDE + c * CH
+            n = HALF if s < HALVED_LOADS else PER_SLAB
+            for first in range(0, PER_SLAB, n):
+                piece = sb.tile([P, PACK, n * CHUNK], F32, name="raw%d_%d" % (s, first), align_bytes=64)
+                col = h * WIDE + first * CHUNK
                 nc.sync.dma_start(
                     out=piece[:],
-                    in_=src[g * K_PASS : (g + 1) * K_PASS, col : col + n * CH].rearrange(
-                        "(p j) c -> p j c", j=PACK
-                    ),
+                    in_=src[g * K_PASS : (g + 1) * K_PASS, col : col + n * CHUNK].rearrange("(p j) c -> p j c", j=PACK),
                 )
                 for i in range(n):
-                    raw[PER * u + c + i] = (piece, i * CH)
-                c = c + n
-            for hh in range(2):
-                if RES_AFTER[hh] == u:
-                    load_res(hh)
+                    raw[PER_SLAB * s + first + i] = (piece, i * CHUNK)
+        res_sb = sb.tile([P, N // P, T], F32, name="res_sb")
+        nc.sync.dma_start(out=res_sb[:], in_=res.rearrange("(i p) t -> p i t", p=P))
 
-        eye = sb.tile([P, P], BF16, name="eye", align_bytes=64)
-        make_identity(nc, eye[:])
-        spread = sb.tile([P, PACK * (K_PASS + 1)], BF16, name="spread", align_bytes=64)
-        nc.vector.memset(spread[:].bitcast(U32), 0)
-        nc.vector.tensor_copy(
-            out=spread[:].rearrange("p (j r) -> p j r", j=PACK)[:, :, 0:K_PASS:PACK],
-            in_=eye[:].unsqueeze(1).to_broadcast([P, PACK, P]),
+        ramp = sb.tile([P, K_PASS], BF16, name="ramp", align_bytes=64)
+        nc.gpsimd.iota(
+            ramp[:], pattern=[[1, K_PASS]], base=0, channel_multiplier=-PACK, allow_small_or_imprecise_dtypes=True
         )
+        eye = sb.tile([P, PACK * K_PASS], BF16, name="eye", align_bytes=64)
+        for j in range(PACK):
+            nc.vector.tensor_scalar(
+                out=eye[:, j * K_PASS : (j + 1) * K_PASS],
+                in0=ramp[:],
+                scalar1=float(j),
+                scalar2=None,
+                op0=mybir.AluOpType.is_equal,
+            )
         eye_codes = sb.tile([P, K_PASS], U32, name="eye_codes", align_bytes=256)
         eye_scales = sb.tile([P, K_PASS], U8, name="eye_scales", align_bytes=256)
         nc.vector.quantize_mx(
-            out=eye_codes[:].bitcast(FMT["q"]), scales=eye_scales[:], in_=spread[:, 0 : PACK * K_PASS]
+            out=eye_codes[:].bitcast(FORMAT["q"]), scales=eye_scales[:], in_=eye[:]
         )
-        if WARM:
-            warm = ps.tile([P, WIDE], F32, name="warm", tag="acc0")
-            for i in range(WARM):
-                nc.tensor.matmul_mx(
-                    out=warm[:], lhsT=eye_codes[:, 0:P].bitcast(FMT["q"]), lhsT_scale=eye_scales[:, 0:P],
-                    rhs=eye_codes[:].bitcast(FMT["q"]), rhs_scale=eye_scales[:], start=True, stop=True,
-                )
 
-        bf = {}
+        rounded = {}
         codes = {}
         scales = {}
-        for u in range(len(UNITS)):
+        for s in range(len(SLABS)):
             for tier in "qr":
-                bf[tier, u] = sb.tile([P, WIDE * PACK], BF16, name="bf_%s%d" % (tier, u), align_bytes=256)
-                codes[tier, u] = sb.tile([P, WIDE], U32, name="codes_%s%d" % (tier, u), align_bytes=256)
-                scales[tier, u] = sb.tile([P, WIDE], U8, name="scales_%s%d" % (tier, u), align_bytes=256)
+                rounded[tier, s] = sb.tile([P, WIDE * PACK], BF16, name="rounded_%s%d" % (tier, s), align_bytes=256)
+                codes[tier, s] = sb.tile([P, WIDE], U32, name="codes_%s%d" % (tier, s), align_bytes=256)
+                scales[tier, s] = sb.tile([P, WIDE], U8, name="scales_%s%d" % (tier, s), align_bytes=256)
 
-        def grouped(tier, c0, n, run):
-            lo = (c0 % PER) * CH * PACK
-            return bf[tier, c0 // PER][:, lo : lo + n * CH * PACK].rearrange("p (c i j) -> p c j i", i=run, j=PACK)
+        def interleaved(tier, first, n):
+            lo = (first % PER_SLAB) * CHUNK * PACK
+            flat = rounded[tier, first // PER_SLAB][:, lo : lo + n * CHUNK * PACK]
+            return flat.rearrange("p (c i j) -> p c j i", i=RUN, j=PACK)
 
-        def rows(c0, n, run):
-            piece, lo = raw[c0]
-            return piece[:, :, lo : lo + n * CH].rearrange("p j (c i) -> p c j i", i=run)
+        def raw_rows(first, n):
+            piece, lo = raw[first]
+            return piece[:, :, lo : lo + n * CHUNK].rearrange("p j (c i) -> p c j i", i=RUN)
 
-        def cast(c0, n):
-            c = c0
-            while c < c0 + n:
-                m = 1
-                while c + m < c0 + n and raw[c + m][0] is raw[c][0]:
-                    m = m + 1
-                if c in VCAST:
-                    nc.vector.tensor_copy(out=grouped("q", c, m, RUN_CAST), in_=rows(c, m, RUN_CAST))
-                else:
-                    nc.scalar.copy(out=grouped("q", c, m, RUN_CAST), in_=rows(c, m, RUN_CAST))
-                c = c + m
+        ready = {}
 
-        def quant(tier, c0, n):
-            u, lo = c0 // PER, (c0 % PER) * CH
+        def quantise(tier, first, n, usable_from):
+            s, lo = first // PER_SLAB, (first % PER_SLAB) * CHUNK
             nc.vector.quantize_mx(
-                out=codes[tier, u][:, lo : lo + n * CH].bitcast(FMT[tier]),
-                scales=scales[tier, u][:, lo : lo + n * CH],
-                in_=bf[tier, u][:, lo * PACK : (lo + n * CH) * PACK],
+                out=codes[tier, s][:, lo : lo + n * CHUNK].bitcast(FORMAT[tier]),
+                scales=scales[tier, s][:, lo : lo + n * CHUNK],
+                in_=rounded[tier, s][:, lo * PACK : (lo + n * CHUNK) * PACK],
             )
+            for c in range(first, first + n):
+                ready[tier, c] = usable_from
+
+        def round_and_quantise(first, n, usable_from):
+            copy = nc.vector.tensor_copy if first == 0 else nc.scalar.copy
+            copy(out=interleaved("q", first, n), in_=raw_rows(first, n))
+            quantise("q", first, n, usable_from)
 
         back = {}
 
-        def dequant(c):
-            u, lo = c // PER, (c % PER) * CH
-            back[c] = ps.tile([P, PACK, CH], F32, name="back%d" % c, tag="back%d" % (c % 4))
+        def dequantise(c):
+            s, lo = c // PER_SLAB, (c % PER_SLAB) * CHUNK
+            back[c] = ps.tile([P, PACK, CHUNK], F32, name="back%d" % c, tag="back%d" % (c % BACK_BANKS))
             for j in range(PACK):
                 nc.tensor.matmul_mx(
                     out=back[c][:, j, :],
-                    lhsT=eye_codes[:, j * P : (j + 1) * P].bitcast(FMT["q"]),
+                    lhsT=eye_codes[:, j * P : (j + 1) * P].bitcast(FORMAT["q"]),
                     lhsT_scale=eye_scales[:, j * P : (j + 1) * P],
-                    rhs=codes["q", u][:, lo : lo + CH].bitcast(FMT["q"]),
-                    rhs_scale=scales["q", u][:, lo : lo + CH],
+                    rhs=codes["q", s][:, lo : lo + CHUNK].bitcast(FORMAT["q"]),
+                    rhs_scale=scales["q", s][:, lo : lo + CHUNK],
                     start=True,
                     stop=True,
                 )
 
-        def sub(c):
+        def subtract(c):
             nc.vector.tensor_tensor(
-                out=grouped("r", c, 1, RUN_SUB),
-                in0=rows(c, 1, RUN_SUB),
-                in1=back[c][:].rearrange("p j (c i) -> p c j i", i=RUN_SUB),
+                out=interleaved("r", c, 1),
+                in0=raw_rows(c, 1),
+                in1=back[c][:].rearrange("p j (c i) -> p c j i", i=RUN),
                 op=mybir.AluOpType.subtract,
             )
 
         acc = {}
+        passes_done = {}
+        closed_at = {}
+        drained = set()
+        parked = {}
+        waiting = [
+            (h, g, i, w_tier, x_tier)
+            for h in range(T // WIDE)
+            for g in range(K // K_PASS)
+            for i in range(N // P)
+            for x_tier in "qr"
+            for w_tier in "qr"
+        ]
 
-        def product(p, start, stop):
-            h, g, t, wt, xt = p
-            xu, wu = UNITS.index(("x", g, h)), UNITS.index(("w", g, 0))
-            if start:
-                acc[h, t] = ps.tile([P, WIDE], F32, name="acc%d_%d" % (h, t), tag="acc%d" % t)
+        def can_run(product, step):
+            h, g, i, w_tier, x_tier = product
+            x_first = PER_SLAB * SLABS.index(("x", g, h))
+            needs = [(w_tier, PER_SLAB * SLABS.index(("w", g, 0)) + i)]
+            needs.extend((x_tier, x_first + c) for c in range(PER_SLAB))
+            bank_free = h == 0 or (h - 1, i) in drained
+            return bank_free and all(need in ready and ready[need] <= step for need in needs)
+
+        def multiply(product, step):
+            h, g, i, w_tier, x_tier = product
+            xs, ws = SLABS.index(("x", g, h)), SLABS.index(("w", g, 0))
+            done = passes_done.get((h, i), 0)
+            if done == 0:
+                acc[h, i] = ps.tile([P, WIDE], F32, name="acc%d_%d" % (h, i), tag="acc%d" % i)
             nc.tensor.matmul_mx(
-                out=acc[h, t][:],
-                lhsT=codes[wt, wu][:, t * P : (t + 1) * P].bitcast(FMT[wt]),
-                lhsT_scale=scales[wt, wu][:, t * P : (t + 1) * P],
-                rhs=codes[xt, xu][:].bitcast(FMT[xt]),
-                rhs_scale=scales[xt, xu][:],
-                start=start,
-                stop=stop,
+                out=acc[h, i][:],
+                lhsT=codes[w_tier, ws][:, i * P : (i + 1) * P].bitcast(FORMAT[w_tier]),
+                lhsT_scale=scales[w_tier, ws][:, i * P : (i + 1) * P],
+                rhs=codes[x_tier, xs][:].bitcast(FORMAT[x_tier]),
+                rhs_scale=scales[x_tier, xs][:],
+                start=done == 0,
+                stop=done == PASSES_PER_TILE - 1,
             )
+            passes_done[h, i] = done + 1
+            if done == PASSES_PER_TILE - 1:
+                closed_at[h, i] = step
+            waiting.remove(product)
 
-        def finish(key):
-            h, t = key
-            parts = LAST_SPLIT if key == (1, PER - 1) else 1
+        def add_and_store(sums, h, i, parts, adder):
             width = WIDE // parts
-            for i in range(parts):
-                cols = slice(i * width, (i + 1) * width)
-                o = sb.tile([P, width], F32, name="o%d_%d_%d" % (h, t, i))
-                nc.vector.tensor_tensor(out=o[:], in0=res_sb[h][:, t, cols], in1=acc[h, t][:, cols], op=mybir.AluOpType.add)
-                eng = nc.scalar if (parts > 1 and i % 2 == 1) else nc.sync
-                eng.dma_start(out=out[t * P : (t + 1) * P, h * WIDE + i * width : h * WIDE + (i + 1) * width], in_=o[:])
+            for part in range(parts):
+                lo = part * width
+                result = sb.tile([P, width], F32, name="result%d_%d_%d" % (h, i, part))
+                cols = slice(h * WIDE + lo, h * WIDE + lo + width)
+                adder.tensor_tensor(
+                    out=result[:], in0=res_sb[:, i, cols], in1=sums[:, lo : lo + width], op=mybir.AluOpType.add
+                )
+                queue = nc.sync if part % 2 == 0 else nc.scalar
+                queue.dma_start(out=out[i * P : (i + 1) * P, cols], in_=result[:])
 
-        ready = {}
-        count = {}
-        todo = [(h, g, t, wt, xt) for h in range(2) for g in range(2) for t in range(PER) for xt in "qr" for wt in "qr"]
-        finished = set()
-        closing = []
+        def group(tier, s):
+            if tier == "q":
+                return 1 if s < 2 else HALF
+            return PER_SLAB if SLABS[s][0] == "x" else HALF
 
-        def can_run(p, step):
-            h, g, t, wt, xt = p
-            if h == 1 and (0, t) not in finished:
-                return False
-            xu, wu = UNITS.index(("x", g, h)), UNITS.index(("w", g, 0))
-            return ready.get((wt, PER * wu + t), 99) <= step and all(
-                ready.get((xt, PER * xu + i), 99) <= step for i in range(PER)
-            )
+        def quantise_step(c):
+            s = c // PER_SLAB
+            return c - c % group("q", s) - min(s + 1, MAX_LEAD)
 
-        def products(n, ready_by, stamp):
-            for i in range(n):
-                cands = [p for p in todo if can_run(p, ready_by)]
-                if not cands:
-                    return
-                p = cands[0]
-                todo.remove(p)
-                key = (p[0], p[2])
-                count[key] = count.get(key, 0) + 1
-                product(p, count[key] == 1, count[key] == 8)
-                if count[key] == 8:
-                    closing.append((stamp, key))
+        for step in range(-1, CHUNKS + 1):
+            for c in range(CHUNKS):
+                n = group("q", c // PER_SLAB)
+                if c % n == 0 and quantise_step(c) == step:
+                    round_and_quantise(c, n, step + 1)
+            if step == PER_SLAB:
+                quantise("r", 0, PER_SLAB, step)
+            for c in range(CHUNKS):
+                if max(quantise_step(c), c - BACK_LEAD) == step:
+                    dequantise(c)
+            if 0 <= step < CHUNKS:
+                subtract(step)
+            if step > PER_SLAB and step % group("r", (step - 1) // PER_SLAB) == 0:
+                n = group("r", (step - 1) // PER_SLAB)
+                quantise("r", step - n, n, step + 1)
+            due = [key for key in closed_at if key not in drained and closed_at[key] + DRAIN_DELAY <= step]
+            if due:
+                h, i = due[0]
+                parked[i] = sb.tile([P, WIDE], F32, name="parked%d" % i)
+                nc.scalar.copy(out=parked[i][:], in_=acc[h, i][:])
+            if step < CHUNKS:
+                for slot in range(PRODUCTS_PER_STEP):
+                    runnable = [product for product in waiting if can_run(product, step)]
+                    if runnable:
+                        multiply(runnable[0], step)
+            if due:
+                drained.add(due[0])
 
-        for step in range(-6, NCH + 20):
-            for c0 in range(NCH):
-                n = QW[c0 // PER]
-                if c0 % n == 0 and QSTEP[c0] == step:
-                    cast(c0, n)
-                    quant("q", c0, n)
-                    for i in range(n):
-                        ready["q", c0 + i] = step
-            for c in range(NCH):
-                if max(QSTEP[c - c % QW[c // PER]], c - LD) == step:
-                    dequant(c)
-            if 0 <= step < NCH:
-                sub(step)
-            fin = [k for s, k in closing if s + FL <= step and k not in finished][: 1 if step < NCH else PER]
-            c = step - 1
-            if 0 <= c < NCH and (c + 1) % RW[c // PER] == 0:
-                n = RW[c // PER]
-                quant("r", c + 1 - n, n)
-                for i in range(n):
-                    ready["r", c + 1 - n + i] = step
-            for k in fin:
-                finish(k)
-            if step >= NCH:
-                todo = sorted(todo, key=lambda p: (p[0], p[2]))
-                products(2, step, step - FL + 1)
-            else:
-                products(BUDF if fin else BUD, step - LAG, step)
-            for k in fin:
-                finished.add(k)
-        assert not todo and len(finished) == 8
+        for i in range(N // P):
+            add_and_store(parked[i], 0, i, 1, nc.vector)
+        for i in range(N // P):
+            for product in [product for product in waiting if product[2] == i]:
+                multiply(product, CHUNKS)
+            add_and_store(acc[1, i], 1, i, 2 if i == N // P - 1 else 1, nc.vector)
+        assert not waiting

@@ -25,12 +25,9 @@ BACK_BANKS = 4
 RUN = 2
 HALVED_LOADS = 3
 MAX_LEAD = 3
-BACK_LEAD = 2
+BACK_LEAD = 3
 PRODUCTS_PER_STEP = 3
 DRAIN_DELAY = 2
-WARM_HEAD = 0
-WARM_EACH = 0
-WARM_UNTIL = 0
 
 
 def tile_mix_tierb_four_res_kernel(tc, w, x, res, out):
@@ -61,7 +58,10 @@ def tile_mix_tierb_four_res_kernel(tc, w, x, res, out):
             ramp[:], pattern=[[1, K_PASS]], base=0, channel_multiplier=-PACK, allow_small_or_imprecise_dtypes=True
         )
         eye = sb.tile([P, PACK * K_PASS], BF16, name="eye", align_bytes=64)
-        for j in range(PACK):
+        eye_codes = sb.tile([P, K_PASS], U32, name="eye_codes", align_bytes=256)
+        eye_scales = sb.tile([P, K_PASS], U8, name="eye_scales", align_bytes=256)
+
+        def mark(j):
             nc.vector.tensor_scalar(
                 out=eye[:, j * K_PASS : (j + 1) * K_PASS],
                 in0=ramp[:],
@@ -69,11 +69,36 @@ def tile_mix_tierb_four_res_kernel(tc, w, x, res, out):
                 scalar2=None,
                 op0=mybir.AluOpType.is_equal,
             )
-        eye_codes = sb.tile([P, K_PASS], U32, name="eye_codes", align_bytes=256)
-        eye_scales = sb.tile([P, K_PASS], U8, name="eye_scales", align_bytes=256)
-        nc.vector.quantize_mx(
-            out=eye_codes[:].bitcast(FORMAT["q"]), scales=eye_scales[:], in_=eye[:]
-        )
+
+        def quantise_eye(lo, hi):
+            nc.vector.quantize_mx(
+                out=eye_codes[:, lo * P : hi * P].bitcast(FORMAT["q"]),
+                scales=eye_scales[:, lo * P : hi * P],
+                in_=eye[:, lo * K_PASS : hi * K_PASS],
+            )
+
+        mark(0)
+        mark(1)
+        quantise_eye(0, 1)
+        mark(2)
+        mark(3)
+        quantise_eye(1, 2)
+        quantise_eye(2, 4)
+        idle = ps.tile([P, CHUNK], F32, name="idle", tag="acc%d" % (PER_SLAB - 1))
+
+        def warm(n):
+            for i in range(n):
+                nc.tensor.matmul_mx(
+                    out=idle[:],
+                    lhsT=eye_codes[:, 0:P].bitcast(FORMAT["q"]),
+                    lhsT_scale=eye_scales[:, 0:P],
+                    rhs=eye_codes[:, 0:P].bitcast(FORMAT["q"]),
+                    rhs_scale=eye_scales[:, 0:P],
+                    start=True,
+                    stop=True,
+                )
+
+        warm(10)
 
         rounded = {}
         codes = {}
@@ -104,11 +129,6 @@ def tile_mix_tierb_four_res_kernel(tc, w, x, res, out):
             )
             for c in range(first, first + n):
                 ready[tier, c] = usable_from
-
-        def round_and_quantise(first, n, usable_from):
-            copy = nc.vector.tensor_copy if first == 0 else nc.scalar.copy
-            copy(out=interleaved("q", first, n), in_=raw_rows(first, n))
-            quantise("q", first, n, usable_from)
 
         back = {}
 
@@ -197,21 +217,29 @@ def tile_mix_tierb_four_res_kernel(tc, w, x, res, out):
             s = c // PER_SLAB
             return c - c % group("q", s) - min(s + 1, MAX_LEAD)
 
+        for c in range(CHUNKS):
+            n = group("q", c // PER_SLAB)
+            if c % n == 0:
+                copy = nc.vector.tensor_copy if c == 0 else nc.scalar.copy
+                copy(out=interleaved("q", c, n), in_=raw_rows(c, n))
+
         for step in range(-1, CHUNKS + 1):
             for c in range(CHUNKS):
                 n = group("q", c // PER_SLAB)
                 if c % n == 0 and quantise_step(c) == step:
-                    round_and_quantise(c, n, step + 1)
+                    quantise("q", c, n, step + 0)
             if step == PER_SLAB:
                 quantise("r", 0, PER_SLAB, step)
             for c in range(CHUNKS):
                 if max(quantise_step(c), c - BACK_LEAD) == step:
                     dequantise(c)
+                    if c == 1:
+                        warm(4)
             if 0 <= step < CHUNKS:
                 subtract(step)
             if step > PER_SLAB and step % group("r", (step - 1) // PER_SLAB) == 0:
                 n = group("r", (step - 1) // PER_SLAB)
-                quantise("r", step - n, n, step + 1)
+                quantise("r", step - n, n, step + 0)
             due = [key for key in closed_at if key not in drained and closed_at[key] + DRAIN_DELAY <= step]
             if due:
                 h, i = due[0]

@@ -50,8 +50,12 @@ def tile_mix_tierb_four_res_kernel(tc, w, x, res, out):
                 )
                 for i in range(n):
                     raw[PER_SLAB * s + first + i] = (piece, i * CHUNK)
-        res_sb = sb.tile([P, N // P, T], F32, name="res_sb")
-        nc.sync.dma_start(out=res_sb[:], in_=res.rearrange("(i p) t -> p i t", p=P))
+        res_sb = {}
+        for h in range(T // WIDE):
+            res_sb[h] = sb.tile([P, N // P, WIDE], F32, name="res%d" % h)
+            nc.sync.dma_start(
+                out=res_sb[h][:], in_=res[:, h * WIDE : (h + 1) * WIDE].rearrange("(i p) t -> p i t", p=P)
+            )
 
         ramp = sb.tile([P, K_PASS], BF16, name="ramp", align_bytes=64)
         nc.gpsimd.iota(
@@ -203,9 +207,9 @@ def tile_mix_tierb_four_res_kernel(tc, w, x, res, out):
                 result = sb.tile([P, width], F32, name="result%d_%d_%d" % (h, i, part))
                 cols = slice(h * WIDE + lo, h * WIDE + lo + width)
                 adder.tensor_tensor(
-                    out=result[:], in0=res_sb[:, i, cols], in1=sums[:, lo : lo + width], op=mybir.AluOpType.add
+                    out=result[:], in0=res_sb[h][:, i, lo : lo + width], in1=sums[:, lo : lo + width], op=mybir.AluOpType.add
                 )
-                queue = nc.sync if part % 2 == 0 else nc.scalar
+                queue = nc.scalar if part == 1 and h == 1 else nc.sync
                 queue.dma_start(out=out[i * P : (i + 1) * P, cols], in_=result[:])
 
         def group(tier, s):
@@ -215,18 +219,19 @@ def tile_mix_tierb_four_res_kernel(tc, w, x, res, out):
 
         def quantise_step(c):
             s = c // PER_SLAB
-            return c - c % group("q", s) - min(s + 1, MAX_LEAD)
+            return c - c % group("q", s) - (2 if s < 2 else MAX_LEAD)
 
         for c in range(CHUNKS):
             n = group("q", c // PER_SLAB)
-            if c % n == 0:
-                copy = nc.vector.tensor_copy if c == 0 else nc.scalar.copy
-                copy(out=interleaved("q", c, n), in_=raw_rows(c, n))
+            if c % n == 0 and c not in (0, HALF):
+                nc.scalar.copy(out=interleaved("q", c, n), in_=raw_rows(c, n))
 
-        for step in range(-1, CHUNKS + 1):
+        for step in range(-2, CHUNKS + 1):
             for c in range(CHUNKS):
                 n = group("q", c // PER_SLAB)
                 if c % n == 0 and quantise_step(c) == step:
+                    if c in (0, HALF):
+                        nc.vector.tensor_copy(out=interleaved("q", c, n), in_=raw_rows(c, n))
                     quantise("q", c, n, step + 0)
             if step == PER_SLAB:
                 quantise("r", 0, PER_SLAB, step)
@@ -245,6 +250,8 @@ def tile_mix_tierb_four_res_kernel(tc, w, x, res, out):
                 h, i = due[0]
                 parked[i] = sb.tile([P, WIDE], F32, name="parked%d" % i)
                 nc.scalar.copy(out=parked[i][:], in_=acc[h, i][:])
+                if i < 3:
+                    add_and_store(parked[i], h, i, 2, nc.gpsimd)
             if step < CHUNKS:
                 for slot in range(PRODUCTS_PER_STEP):
                     runnable = [product for product in waiting if can_run(product, step)]
@@ -253,7 +260,7 @@ def tile_mix_tierb_four_res_kernel(tc, w, x, res, out):
             if due:
                 drained.add(due[0])
 
-        for i in range(N // P):
+        for i in range(3, N // P):
             add_and_store(parked[i], 0, i, 1, nc.vector)
         for i in range(N // P):
             for product in [product for product in waiting if product[2] == i]:

@@ -17,39 +17,53 @@ K_PASS = P * PACK
 WIDE = 512
 CHUNK = 128
 PER_SLAB = WIDE // CHUNK
-HALF = PER_SLAB // 2
-SLABS = [("x", 0, 0), ("w", 0, 0), ("x", 1, 0), ("w", 1, 0), ("x", 0, 1), ("x", 1, 1)]
-CHUNKS = PER_SLAB * len(SLABS)
-PASSES_PER_TILE = 4 * (K // K_PASS)
-BACK_BANKS = 4
 RUN = 2
-HALVED_LOADS = 3
-MAX_LEAD = 3
-BACK_LEAD = 3
+PASSES_PER_TILE = 4 * (K // K_PASS)
+LOADS = (
+    [("x", 0, 0, first, 2) for first in (0, 2)]
+    + [("w", 0, 0, first, 1) for first in range(4)]
+    + [(kind, 1, 0, first, 2) for kind in "xw" for first in (0, 2)]
+    + [("x", 0, 1, 0, 4), ("x", 1, 1, 0, 4)]
+)
+BACK_BANKS = 4
+HEAD = 8
+HEAD_LEAD = 4
+LEAD = 3
+BACK_LEAD = 4
 PRODUCTS_PER_STEP = 3
+PRODUCT_LAG = 0
 DRAIN_DELAY = 2
+GPSIMD_TILES = 2
+VECTOR_CASTS = (0, 2)
+WARM = 10
+URGENT = (3, 11, 19, 23)
+Q_FIRST = 0
+LATE = (3, 11, 19, 23)
+BY_AGE = 8
 
 
 def tile_mix_tierb_four_res_kernel(tc, w, x, res, out):
     nc = tc.nc
+    acc_banks = 8 - BACK_BANKS
     with ExitStack() as ctx:
         sb = ctx.enter_context(tc.tile_pool(name="sb", bufs=1))
         ps = ctx.enter_context(tc.psum_pool(name="ps", bufs=1))
         ctx.enter_context(tc.manual_schedule())
 
         raw = {}
-        for s, (kind, g, h) in enumerate(SLABS):
+        order = []
+        for number, (kind, g, h, first, n) in enumerate(LOADS):
             src = x if kind == "x" else w
-            n = HALF if s < HALVED_LOADS else PER_SLAB
-            for first in range(0, PER_SLAB, n):
-                piece = sb.tile([P, PACK, n * CHUNK], F32, name="raw%d_%d" % (s, first), align_bytes=64)
-                col = h * WIDE + first * CHUNK
-                nc.sync.dma_start(
-                    out=piece[:],
-                    in_=src[g * K_PASS : (g + 1) * K_PASS, col : col + n * CHUNK].rearrange("(p j) c -> p j c", j=PACK),
-                )
-                for i in range(n):
-                    raw[PER_SLAB * s + first + i] = (piece, i * CHUNK)
+            piece = sb.tile([P, PACK, n * CHUNK], F32, name="raw%d" % number, align_bytes=64)
+            col = h * WIDE + first * CHUNK
+            nc.sync.dma_start(
+                out=piece[:],
+                in_=src[g * K_PASS : (g + 1) * K_PASS, col : col + n * CHUNK].rearrange("(p j) c -> p j c", j=PACK),
+            )
+            for i in range(n):
+                raw[len(order)] = (piece, i * CHUNK)
+                order.append(((kind, g, h), first + i))
+        chunks = len(order)
         res_sb = {}
         for h in range(T // WIDE):
             res_sb[h] = sb.tile([P, N // P, WIDE], F32, name="res%d" % h)
@@ -88,67 +102,70 @@ def tile_mix_tierb_four_res_kernel(tc, w, x, res, out):
         mark(3)
         quantise_eye(1, 2)
         quantise_eye(2, 4)
-        idle = ps.tile([P, CHUNK], F32, name="idle", tag="acc%d" % (PER_SLAB - 1))
-
-        def warm(n):
-            for i in range(n):
-                nc.tensor.matmul_mx(
-                    out=idle[:],
-                    lhsT=eye_codes[:, 0:P].bitcast(FORMAT["q"]),
-                    lhsT_scale=eye_scales[:, 0:P],
-                    rhs=eye_codes[:, 0:P].bitcast(FORMAT["q"]),
-                    rhs_scale=eye_scales[:, 0:P],
-                    start=True,
-                    stop=True,
-                )
-
-        warm(10)
+        idle = ps.tile([P, CHUNK], F32, name="idle", tag="acc%d" % (acc_banks - 1))
+        for i in range(WARM):
+            nc.tensor.matmul_mx(
+                out=idle[:],
+                lhsT=eye_codes[:, 0:P].bitcast(FORMAT["q"]),
+                lhsT_scale=eye_scales[:, 0:P],
+                rhs=eye_codes[:, 0:P].bitcast(FORMAT["q"]),
+                rhs_scale=eye_scales[:, 0:P],
+                start=True,
+                stop=True,
+            )
 
         rounded = {}
         codes = {}
         scales = {}
-        for s in range(len(SLABS)):
+        for slab in sorted(set(slab for slab, i in order)):
             for tier in "qr":
-                rounded[tier, s] = sb.tile([P, WIDE * PACK], BF16, name="rounded_%s%d" % (tier, s), align_bytes=256)
-                codes[tier, s] = sb.tile([P, WIDE], U32, name="codes_%s%d" % (tier, s), align_bytes=256)
-                scales[tier, s] = sb.tile([P, WIDE], U8, name="scales_%s%d" % (tier, s), align_bytes=256)
+                label = "%s_%s%d%d" % ((tier,) + slab)
+                rounded[tier, slab] = sb.tile([P, WIDE * PACK], BF16, name="rounded" + label, align_bytes=256)
+                codes[tier, slab] = sb.tile([P, WIDE], U32, name="codes" + label, align_bytes=256)
+                scales[tier, slab] = sb.tile([P, WIDE], U8, name="scales" + label, align_bytes=256)
 
-        def interleaved(tier, first, n):
-            lo = (first % PER_SLAB) * CHUNK * PACK
-            flat = rounded[tier, first // PER_SLAB][:, lo : lo + n * CHUNK * PACK]
+        def interleaved(tier, c, n):
+            slab, i = order[c]
+            flat = rounded[tier, slab][:, i * CHUNK * PACK : (i + n) * CHUNK * PACK]
             return flat.rearrange("p (c i j) -> p c j i", i=RUN, j=PACK)
 
-        def raw_rows(first, n):
-            piece, lo = raw[first]
+        def raw_rows(c, n):
+            piece, lo = raw[c]
             return piece[:, :, lo : lo + n * CHUNK].rearrange("p j (c i) -> p c j i", i=RUN)
 
         ready = {}
+        made = {}
 
-        def quantise(tier, first, n, usable_from):
-            s, lo = first // PER_SLAB, (first % PER_SLAB) * CHUNK
+        def quantise(tier, c, n, step):
+            slab, i = order[c]
+            lo = i * CHUNK
             nc.vector.quantize_mx(
-                out=codes[tier, s][:, lo : lo + n * CHUNK].bitcast(FORMAT[tier]),
-                scales=scales[tier, s][:, lo : lo + n * CHUNK],
-                in_=rounded[tier, s][:, lo * PACK : (lo + n * CHUNK) * PACK],
+                out=codes[tier, slab][:, lo : lo + n * CHUNK].bitcast(FORMAT[tier]),
+                scales=scales[tier, slab][:, lo : lo + n * CHUNK],
+                in_=rounded[tier, slab][:, lo * PACK : (lo + n * CHUNK) * PACK],
             )
-            for c in range(first, first + n):
-                ready[tier, c] = usable_from
+            for m in range(n):
+                ready[tier, slab, i + m] = step + (PRODUCT_LAG if tier == "r" else 0)
+                made[tier, slab, i + m] = len(made)
 
         back = {}
 
-        def dequantise(c):
-            s, lo = c // PER_SLAB, (c % PER_SLAB) * CHUNK
-            back[c] = ps.tile([P, PACK, CHUNK], F32, name="back%d" % c, tag="back%d" % (c % BACK_BANKS))
+        def dequantise(first, n):
+            for c in range(first, first + n):
+                back[c] = ps.tile([P, PACK, CHUNK], F32, name="back%d" % c, tag="back%d" % (c % BACK_BANKS))
             for j in range(PACK):
-                nc.tensor.matmul_mx(
-                    out=back[c][:, j, :],
-                    lhsT=eye_codes[:, j * P : (j + 1) * P].bitcast(FORMAT["q"]),
-                    lhsT_scale=eye_scales[:, j * P : (j + 1) * P],
-                    rhs=codes["q", s][:, lo : lo + CHUNK].bitcast(FORMAT["q"]),
-                    rhs_scale=scales["q", s][:, lo : lo + CHUNK],
-                    start=True,
-                    stop=True,
-                )
+                for c in range(first, first + n):
+                    slab, i = order[c]
+                    lo = i * CHUNK
+                    nc.tensor.matmul_mx(
+                        out=back[c][:, j, :],
+                        lhsT=eye_codes[:, j * P : (j + 1) * P].bitcast(FORMAT["q"]),
+                        lhsT_scale=eye_scales[:, j * P : (j + 1) * P],
+                        rhs=codes["q", slab][:, lo : lo + CHUNK].bitcast(FORMAT["q"]),
+                        rhs_scale=scales["q", slab][:, lo : lo + CHUNK],
+                        start=True,
+                        stop=True,
+                    )
 
         def subtract(c):
             nc.vector.tensor_tensor(
@@ -163,29 +180,34 @@ def tile_mix_tierb_four_res_kernel(tc, w, x, res, out):
         closed_at = {}
         drained = set()
         parked = {}
+        tiles = N // P
         waiting = [
             (h, g, i, w_tier, x_tier)
             for h in range(T // WIDE)
             for g in range(K // K_PASS)
-            for i in range(N // P)
-            for x_tier in "qr"
+            for i in range(tiles)
             for w_tier in "qr"
+            for x_tier in "qr"
         ]
 
         def can_run(product, step):
             h, g, i, w_tier, x_tier = product
-            x_first = PER_SLAB * SLABS.index(("x", g, h))
-            needs = [(w_tier, PER_SLAB * SLABS.index(("w", g, 0)) + i)]
-            needs.extend((x_tier, x_first + c) for c in range(PER_SLAB))
-            bank_free = h == 0 or (h - 1, i) in drained
+            needs = [(w_tier, ("w", g, 0), i)]
+            needs.extend((x_tier, ("x", g, h), c) for c in range(PER_SLAB))
+            before = h * tiles + i - acc_banks
+            bank_free = before < 0 or divmod(before, tiles) in drained
             return bank_free and all(need in ready and ready[need] <= step for need in needs)
+
+        def age(product):
+            h, g, i, w_tier, x_tier = product
+            return max(made[w_tier, ("w", g, 0), i], made[x_tier, ("x", g, h), PER_SLAB - 1])
 
         def multiply(product, step):
             h, g, i, w_tier, x_tier = product
-            xs, ws = SLABS.index(("x", g, h)), SLABS.index(("w", g, 0))
+            xs, ws = ("x", g, h), ("w", g, 0)
             done = passes_done.get((h, i), 0)
             if done == 0:
-                acc[h, i] = ps.tile([P, WIDE], F32, name="acc%d_%d" % (h, i), tag="acc%d" % i)
+                acc[h, i] = ps.tile([P, WIDE], F32, name="acc%d_%d" % (h, i), tag="acc%d" % ((h * tiles + i) % acc_banks))
             nc.tensor.matmul_mx(
                 out=acc[h, i][:],
                 lhsT=codes[w_tier, ws][:, i * P : (i + 1) * P].bitcast(FORMAT[w_tier]),
@@ -212,58 +234,74 @@ def tile_mix_tierb_four_res_kernel(tc, w, x, res, out):
                 queue = nc.scalar if part == 1 and h == 1 else nc.sync
                 queue.dma_start(out=out[i * P : (i + 1) * P, cols], in_=result[:])
 
-        def group(tier, s):
-            if tier == "q":
-                return 1 if s < 2 else HALF
-            return PER_SLAB if SLABS[s][0] == "x" else HALF
+        def paired(c):
+            return c + 1 < chunks and raw[c][0] is raw[c + 1][0] and order[c][1] % 2 == 0
 
-        def quantise_step(c):
-            s = c // PER_SLAB
-            return c - c % group("q", s) - (2 if s < 2 else MAX_LEAD)
+        def q_group(c):
+            if c >= HEAD and paired(c):
+                return 2
+            if c > HEAD and paired(c - 1):
+                return 0
+            return 1
 
-        for c in range(CHUNKS):
-            n = group("q", c // PER_SLAB)
-            if c % n == 0 and c not in (0, HALF):
+        def q_step(c):
+            return c - (HEAD_LEAD if c < HEAD else LEAD)
+
+        def r_group(c):
+            slab, i = order[c]
+            if slab[0] == "w" or c in URGENT or c + 1 in URGENT:
+                return 1
+            return 2 if i % 2 == 1 else 0
+
+        for c in range(chunks):
+            n = q_group(c)
+            if n and c not in VECTOR_CASTS:
                 nc.scalar.copy(out=interleaved("q", c, n), in_=raw_rows(c, n))
 
-        for step in range(-2, CHUNKS + 1):
-            for c in range(CHUNKS):
-                n = group("q", c // PER_SLAB)
-                if c % n == 0 and quantise_step(c) == step:
-                    if c in (0, HALF):
-                        nc.vector.tensor_copy(out=interleaved("q", c, n), in_=raw_rows(c, n))
-                    quantise("q", c, n, step + 0)
-            if step == PER_SLAB:
-                quantise("r", 0, PER_SLAB, step)
-            for c in range(CHUNKS):
-                if max(quantise_step(c), c - BACK_LEAD) == step:
-                    dequantise(c)
-                    if c == 1:
-                        warm(4)
-            if 0 <= step < CHUNKS:
+        q_at = {}
+        for step in range(-4, chunks + 1):
+            if 0 <= step < chunks and step >= Q_FIRST:
                 subtract(step)
-            if step > PER_SLAB and step % group("r", (step - 1) // PER_SLAB) == 0:
-                n = group("r", (step - 1) // PER_SLAB)
-                quantise("r", step - n, n, step + 0)
-            due = [key for key in closed_at if key not in drained and closed_at[key] + DRAIN_DELAY <= step]
+            for c in range(chunks):
+                n = q_group(c)
+                if n and q_step(c) == step:
+                    if c in VECTOR_CASTS:
+                        nc.vector.tensor_copy(out=interleaved("q", c, n), in_=raw_rows(c, n))
+                    quantise("q", c, n, step)
+                    for m in range(n):
+                        q_at[c + m] = step
+            if 0 <= step < Q_FIRST and step < chunks:
+                subtract(step)
+            for c in (step - 1, step):
+                if c in LATE or c + 1 in LATE or c + 2 in LATE:
+                    if c == step and c in LATE:
+                        quantise("r", c - 3, 2, step)
+                        quantise("r", c - 1, 2, step)
+                elif 0 <= c < chunks and (c in URGENT) == (c == step) and r_group(c):
+                    quantise("r", c - r_group(c) + 1, r_group(c), step)
+            for c in range(chunks):
+                n = q_group(c)
+                if n and c in q_at and max(q_at[c], c - BACK_LEAD) == step:
+                    dequantise(c, n)
+            due = [key for key in closed_at if key not in drained and closed_at[key] + DRAIN_DELAY <= step and key[0] == 0]
             if due:
                 h, i = due[0]
                 parked[i] = sb.tile([P, WIDE], F32, name="parked%d" % i)
                 nc.scalar.copy(out=parked[i][:], in_=acc[h, i][:])
-                if i < 3:
+                if i < GPSIMD_TILES:
                     add_and_store(parked[i], h, i, 2, nc.gpsimd)
-            if step < CHUNKS:
+            if step < chunks:
                 for slot in range(PRODUCTS_PER_STEP):
                     runnable = [product for product in waiting if can_run(product, step)]
                     if runnable:
-                        multiply(runnable[0], step)
+                        multiply(min(runnable, key=age) if step < BY_AGE else runnable[0], step)
             if due:
                 drained.add(due[0])
 
-        for i in range(3, N // P):
+        for i in range(GPSIMD_TILES, tiles):
             add_and_store(parked[i], 0, i, 1, nc.vector)
-        for i in range(N // P):
+        for i in range(tiles):
             for product in [product for product in waiting if product[2] == i]:
-                multiply(product, CHUNKS)
-            add_and_store(acc[1, i], 1, i, 2 if i == N // P - 1 else 1, nc.vector)
+                multiply(product, chunks)
+            add_and_store(acc[1, i], 1, i, 2 if i == tiles - 1 else 1, nc.vector)
         assert not waiting

@@ -19,27 +19,24 @@ CHUNK = 128
 PER_SLAB = WIDE // CHUNK
 RUN = 2
 PASSES_PER_TILE = 4 * (K // K_PASS)
-LOADS = (
-    [("x", 0, 0, first, 2) for first in (0, 2)]
-    + [("w", 0, 0, first, 1) for first in range(4)]
-    + [(kind, 1, 0, first, 2) for kind in "xw" for first in (0, 2)]
-    + [("x", 0, 1, 0, 4), ("x", 1, 1, 0, 4)]
-)
+SLABS = [("x", 0, 0), ("w", 0, 0), ("x", 1, 0), ("w", 1, 0), ("x", 0, 1), ("x", 1, 1)]
+LOADS = [slab + (first, 2) for slab in SLABS for first in (0, 2)]
 BACK_BANKS = 4
 HEAD = 8
-HEAD_LEAD = 4
+HEAD_LEAD = 3
 LEAD = 3
 BACK_LEAD = 4
 PRODUCTS_PER_STEP = 3
 PRODUCT_LAG = 0
 DRAIN_DELAY = 2
-GPSIMD_TILES = 2
+GPSIMD_TILES = 0
 VECTOR_CASTS = (0, 2)
 WARM = 10
 URGENT = (3, 11, 19, 23)
 Q_FIRST = 0
 LATE = (3, 11, 19, 23)
 BY_AGE = 8
+CAST_LEAD = 2
 
 
 def tile_mix_tierb_four_res_kernel(tc, w, x, res, out):
@@ -253,13 +250,13 @@ def tile_mix_tierb_four_res_kernel(tc, w, x, res, out):
                 return 1
             return 2 if i % 2 == 1 else 0
 
-        for c in range(chunks):
-            n = q_group(c)
-            if n and c not in VECTOR_CASTS:
-                nc.scalar.copy(out=interleaved("q", c, n), in_=raw_rows(c, n))
 
         q_at = {}
-        for step in range(-4, chunks + 1):
+        for step in range(-4 - CAST_LEAD, chunks + 1):
+            for c in range(chunks):
+                n = q_group(c)
+                if n and c not in VECTOR_CASTS and q_step(c) - CAST_LEAD == step:
+                    nc.scalar.copy(out=interleaved("q", c, n), in_=raw_rows(c, n))
             if 0 <= step < chunks and step >= Q_FIRST:
                 subtract(step)
             for c in range(chunks):

@@ -17,53 +17,45 @@ K_PASS = P * PACK
 WIDE = 512
 CHUNK = 128
 PER_SLAB = WIDE // CHUNK
-RUN = 2
+TILES = N // P
+BACK_BANKS = 8 - TILES
 PASSES_PER_TILE = 4 * (K // K_PASS)
+RUN = 2
+
 SLABS = [("x", 0, 0), ("w", 0, 0), ("x", 1, 0), ("w", 1, 0), ("x", 0, 1), ("x", 1, 1)]
-LOADS = [slab + (first, 2) for slab in SLABS for first in (0, 2)]
-BACK_BANKS = 4
-HEAD = 8
-HEAD_LEAD = 3
-LEAD = 3
-BACK_LEAD = 4
+CHUNKS = PER_SLAB * len(SLABS)
+HEAD = 2 * PER_SLAB
+LEAD = BACK_BANKS - 1
+ROUND_LEAD = 3
 PRODUCTS_PER_STEP = 3
-PRODUCT_LAG = 0
 DRAIN_DELAY = 2
-GPSIMD_TILES = 0
-VECTOR_CASTS = (0, 2)
-WARM = 10
-URGENT = (3, 11, 19, 23)
-Q_FIRST = 0
-LATE = (3, 11, 19, 23)
-BY_AGE = 8
-CAST_LEAD = 2
+WARM_UP_PASSES = 10
 
 
 def tile_mix_tierb_four_res_kernel(tc, w, x, res, out):
     nc = tc.nc
-    acc_banks = 8 - BACK_BANKS
     with ExitStack() as ctx:
         sb = ctx.enter_context(tc.tile_pool(name="sb", bufs=1))
         ps = ctx.enter_context(tc.psum_pool(name="ps", bufs=1))
         ctx.enter_context(tc.manual_schedule())
 
+        groups = [(c, 1) for c in range(HEAD)] + [(c, 2) for c in range(HEAD, CHUNKS, 2)]
+
         raw = {}
-        order = []
-        for number, (kind, g, h, first, n) in enumerate(LOADS):
+        for first, count in [(0, 2)] + groups[2:]:
+            kind, g, h = SLABS[first // PER_SLAB]
             src = x if kind == "x" else w
-            piece = sb.tile([P, PACK, n * CHUNK], F32, name="raw%d" % number, align_bytes=64)
-            col = h * WIDE + first * CHUNK
+            piece = sb.tile([P, PACK, count * CHUNK], F32, name="raw%d" % first, align_bytes=64)
+            col = h * WIDE + (first % PER_SLAB) * CHUNK
             nc.sync.dma_start(
                 out=piece[:],
-                in_=src[g * K_PASS : (g + 1) * K_PASS, col : col + n * CHUNK].rearrange("(p j) c -> p j c", j=PACK),
+                in_=src[g * K_PASS : (g + 1) * K_PASS, col : col + count * CHUNK].rearrange("(p j) c -> p j c", j=PACK),
             )
-            for i in range(n):
-                raw[len(order)] = (piece, i * CHUNK)
-                order.append(((kind, g, h), first + i))
-        chunks = len(order)
+            for i in range(count):
+                raw[first + i] = (piece, i * CHUNK)
         res_sb = {}
         for h in range(T // WIDE):
-            res_sb[h] = sb.tile([P, N // P, WIDE], F32, name="res%d" % h)
+            res_sb[h] = sb.tile([P, TILES, WIDE], F32, name="res%d" % h)
             nc.sync.dma_start(
                 out=res_sb[h][:], in_=res[:, h * WIDE : (h + 1) * WIDE].rearrange("(i p) t -> p i t", p=P)
             )
@@ -99,8 +91,8 @@ def tile_mix_tierb_four_res_kernel(tc, w, x, res, out):
         mark(3)
         quantise_eye(1, 2)
         quantise_eye(2, 4)
-        idle = ps.tile([P, CHUNK], F32, name="idle", tag="acc%d" % (acc_banks - 1))
-        for i in range(WARM):
+        idle = ps.tile([P, CHUNK], F32, name="idle", tag="acc%d" % (TILES - 1))
+        for i in range(WARM_UP_PASSES):
             nc.tensor.matmul_mx(
                 out=idle[:],
                 lhsT=eye_codes[:, 0:P].bitcast(FORMAT["q"]),
@@ -114,52 +106,47 @@ def tile_mix_tierb_four_res_kernel(tc, w, x, res, out):
         rounded = {}
         codes = {}
         scales = {}
-        for slab in sorted(set(slab for slab, i in order)):
+        for s in range(len(SLABS)):
             for tier in "qr":
-                label = "%s_%s%d%d" % ((tier,) + slab)
-                rounded[tier, slab] = sb.tile([P, WIDE * PACK], BF16, name="rounded" + label, align_bytes=256)
-                codes[tier, slab] = sb.tile([P, WIDE], U32, name="codes" + label, align_bytes=256)
-                scales[tier, slab] = sb.tile([P, WIDE], U8, name="scales" + label, align_bytes=256)
+                rounded[tier, s] = sb.tile([P, WIDE * PACK], BF16, name="rounded_%s%d" % (tier, s), align_bytes=256)
+                codes[tier, s] = sb.tile([P, WIDE], U32, name="codes_%s%d" % (tier, s), align_bytes=256)
+                scales[tier, s] = sb.tile([P, WIDE], U8, name="scales_%s%d" % (tier, s), align_bytes=256)
 
-        def interleaved(tier, c, n):
-            slab, i = order[c]
-            flat = rounded[tier, slab][:, i * CHUNK * PACK : (i + n) * CHUNK * PACK]
+        def interleaved(tier, first, count):
+            lo = (first % PER_SLAB) * CHUNK * PACK
+            flat = rounded[tier, first // PER_SLAB][:, lo : lo + count * CHUNK * PACK]
             return flat.rearrange("p (c i j) -> p c j i", i=RUN, j=PACK)
 
-        def raw_rows(c, n):
-            piece, lo = raw[c]
-            return piece[:, :, lo : lo + n * CHUNK].rearrange("p j (c i) -> p c j i", i=RUN)
+        def raw_rows(first, count):
+            piece, lo = raw[first]
+            return piece[:, :, lo : lo + count * CHUNK].rearrange("p j (c i) -> p c j i", i=RUN)
 
-        ready = {}
         made = {}
 
-        def quantise(tier, c, n, step):
-            slab, i = order[c]
-            lo = i * CHUNK
+        def quantise(tier, first, count):
+            s, lo = first // PER_SLAB, (first % PER_SLAB) * CHUNK
             nc.vector.quantize_mx(
-                out=codes[tier, slab][:, lo : lo + n * CHUNK].bitcast(FORMAT[tier]),
-                scales=scales[tier, slab][:, lo : lo + n * CHUNK],
-                in_=rounded[tier, slab][:, lo * PACK : (lo + n * CHUNK) * PACK],
+                out=codes[tier, s][:, lo : lo + count * CHUNK].bitcast(FORMAT[tier]),
+                scales=scales[tier, s][:, lo : lo + count * CHUNK],
+                in_=rounded[tier, s][:, lo * PACK : (lo + count * CHUNK) * PACK],
             )
-            for m in range(n):
-                ready[tier, slab, i + m] = step + (PRODUCT_LAG if tier == "r" else 0)
-                made[tier, slab, i + m] = len(made)
+            for c in range(first, first + count):
+                made[tier, c] = len(made)
 
         back = {}
 
-        def dequantise(first, n):
-            for c in range(first, first + n):
+        def bring_back(first, count):
+            for c in range(first, first + count):
                 back[c] = ps.tile([P, PACK, CHUNK], F32, name="back%d" % c, tag="back%d" % (c % BACK_BANKS))
             for j in range(PACK):
-                for c in range(first, first + n):
-                    slab, i = order[c]
-                    lo = i * CHUNK
+                for c in range(first, first + count):
+                    s, lo = c // PER_SLAB, (c % PER_SLAB) * CHUNK
                     nc.tensor.matmul_mx(
                         out=back[c][:, j, :],
                         lhsT=eye_codes[:, j * P : (j + 1) * P].bitcast(FORMAT["q"]),
                         lhsT_scale=eye_scales[:, j * P : (j + 1) * P],
-                        rhs=codes["q", slab][:, lo : lo + CHUNK].bitcast(FORMAT["q"]),
-                        rhs_scale=scales["q", slab][:, lo : lo + CHUNK],
+                        rhs=codes["q", s][:, lo : lo + CHUNK].bitcast(FORMAT["q"]),
+                        rhs_scale=scales["q", s][:, lo : lo + CHUNK],
                         start=True,
                         stop=True,
                     )
@@ -175,36 +162,35 @@ def tile_mix_tierb_four_res_kernel(tc, w, x, res, out):
         acc = {}
         passes_done = {}
         closed_at = {}
-        drained = set()
         parked = {}
-        tiles = N // P
         waiting = [
             (h, g, i, w_tier, x_tier)
             for h in range(T // WIDE)
             for g in range(K // K_PASS)
-            for i in range(tiles)
+            for i in range(TILES)
             for w_tier in "qr"
             for x_tier in "qr"
         ]
 
-        def can_run(product, step):
+        def operands(product):
             h, g, i, w_tier, x_tier = product
-            needs = [(w_tier, ("w", g, 0), i)]
-            needs.extend((x_tier, ("x", g, h), c) for c in range(PER_SLAB))
-            before = h * tiles + i - acc_banks
-            bank_free = before < 0 or divmod(before, tiles) in drained
-            return bank_free and all(need in ready and ready[need] <= step for need in needs)
+            w_chunk = PER_SLAB * SLABS.index(("w", g, 0)) + i
+            x_last = PER_SLAB * SLABS.index(("x", g, h)) + PER_SLAB - 1
+            return (w_tier, w_chunk), (x_tier, x_last)
+
+        def can_run(product):
+            h, i = product[0], product[2]
+            return (h == 0 or i in parked) and all(operand in made for operand in operands(product))
 
         def age(product):
-            h, g, i, w_tier, x_tier = product
-            return max(made[w_tier, ("w", g, 0), i], made[x_tier, ("x", g, h), PER_SLAB - 1])
+            return max(made[operand] for operand in operands(product))
 
         def multiply(product, step):
             h, g, i, w_tier, x_tier = product
-            xs, ws = ("x", g, h), ("w", g, 0)
+            xs, ws = SLABS.index(("x", g, h)), SLABS.index(("w", g, 0))
             done = passes_done.get((h, i), 0)
             if done == 0:
-                acc[h, i] = ps.tile([P, WIDE], F32, name="acc%d_%d" % (h, i), tag="acc%d" % ((h * tiles + i) % acc_banks))
+                acc[h, i] = ps.tile([P, WIDE], F32, name="acc%d_%d" % (h, i), tag="acc%d" % i)
             nc.tensor.matmul_mx(
                 out=acc[h, i][:],
                 lhsT=codes[w_tier, ws][:, i * P : (i + 1) * P].bitcast(FORMAT[w_tier]),
@@ -219,86 +205,57 @@ def tile_mix_tierb_four_res_kernel(tc, w, x, res, out):
                 closed_at[h, i] = step
             waiting.remove(product)
 
-        def add_and_store(sums, h, i, parts, adder):
+        def add_and_store(sums, h, i, parts):
             width = WIDE // parts
             for part in range(parts):
                 lo = part * width
                 result = sb.tile([P, width], F32, name="result%d_%d_%d" % (h, i, part))
-                cols = slice(h * WIDE + lo, h * WIDE + lo + width)
-                adder.tensor_tensor(
-                    out=result[:], in0=res_sb[h][:, i, lo : lo + width], in1=sums[:, lo : lo + width], op=mybir.AluOpType.add
+                nc.vector.tensor_tensor(
+                    out=result[:],
+                    in0=res_sb[h][:, i, lo : lo + width],
+                    in1=sums[:, lo : lo + width],
+                    op=mybir.AluOpType.add,
                 )
-                queue = nc.scalar if part == 1 and h == 1 else nc.sync
-                queue.dma_start(out=out[i * P : (i + 1) * P, cols], in_=result[:])
+                queue = nc.sync if part == 0 else nc.scalar
+                queue.dma_start(
+                    out=out[i * P : (i + 1) * P, h * WIDE + lo : h * WIDE + lo + width], in_=result[:]
+                )
 
-        def paired(c):
-            return c + 1 < chunks and raw[c][0] is raw[c + 1][0] and order[c][1] % 2 == 0
-
-        def q_group(c):
-            if c >= HEAD and paired(c):
-                return 2
-            if c > HEAD and paired(c - 1):
-                return 0
-            return 1
-
-        def q_step(c):
-            return c - (HEAD_LEAD if c < HEAD else LEAD)
-
-        def r_group(c):
-            slab, i = order[c]
-            if slab[0] == "w" or c in URGENT or c + 1 in URGENT:
-                return 1
-            return 2 if i % 2 == 1 else 0
-
-
-        q_at = {}
-        for step in range(-4 - CAST_LEAD, chunks + 1):
-            for c in range(chunks):
-                n = q_group(c)
-                if n and c not in VECTOR_CASTS and q_step(c) - CAST_LEAD == step:
-                    nc.scalar.copy(out=interleaved("q", c, n), in_=raw_rows(c, n))
-            if 0 <= step < chunks and step >= Q_FIRST:
+        for step in range(-LEAD - ROUND_LEAD, CHUNKS + 1):
+            for first, count in groups[1:]:
+                if first - LEAD - ROUND_LEAD == step:
+                    nc.scalar.copy(out=interleaved("q", first, count), in_=raw_rows(first, count))
+            if step == -LEAD:
+                nc.vector.tensor_copy(out=interleaved("q", 0, 1), in_=raw_rows(0, 1))
+            if 0 <= step < CHUNKS:
                 subtract(step)
-            for c in range(chunks):
-                n = q_group(c)
-                if n and q_step(c) == step:
-                    if c in VECTOR_CASTS:
-                        nc.vector.tensor_copy(out=interleaved("q", c, n), in_=raw_rows(c, n))
-                    quantise("q", c, n, step)
-                    for m in range(n):
-                        q_at[c + m] = step
-            if 0 <= step < Q_FIRST and step < chunks:
-                subtract(step)
-            for c in (step - 1, step):
-                if c in LATE or c + 1 in LATE or c + 2 in LATE:
-                    if c == step and c in LATE:
-                        quantise("r", c - 3, 2, step)
-                        quantise("r", c - 1, 2, step)
-                elif 0 <= c < chunks and (c in URGENT) == (c == step) and r_group(c):
-                    quantise("r", c - r_group(c) + 1, r_group(c), step)
-            for c in range(chunks):
-                n = q_group(c)
-                if n and c in q_at and max(q_at[c], c - BACK_LEAD) == step:
-                    dequantise(c, n)
-            due = [key for key in closed_at if key not in drained and closed_at[key] + DRAIN_DELAY <= step and key[0] == 0]
+            ahead = [group for group in groups if group[0] - LEAD == step]
+            for group in ahead:
+                quantise("q", *group)
+            if step >= 1 and SLABS[(step - 1) // PER_SLAB][0] == "w":
+                quantise("r", step - 1, 1)
+            if 0 <= step < CHUNKS and SLABS[step // PER_SLAB][0] == "x" and step % PER_SLAB == PER_SLAB - 1:
+                quantise("r", step - 3, 2)
+                quantise("r", step - 1, 2)
+            for group in ahead:
+                bring_back(*group)
+            due = [i for h, i in closed_at if h == 0 and i not in parked and closed_at[h, i] + DRAIN_DELAY <= step]
+            sums = None
             if due:
-                h, i = due[0]
-                parked[i] = sb.tile([P, WIDE], F32, name="parked%d" % i)
-                nc.scalar.copy(out=parked[i][:], in_=acc[h, i][:])
-                if i < GPSIMD_TILES:
-                    add_and_store(parked[i], h, i, 2, nc.gpsimd)
-            if step < chunks:
+                sums = sb.tile([P, WIDE], F32, name="parked%d" % due[0])
+                nc.scalar.copy(out=sums[:], in_=acc[0, due[0]][:])
+            if step < CHUNKS:
                 for slot in range(PRODUCTS_PER_STEP):
-                    runnable = [product for product in waiting if can_run(product, step)]
+                    runnable = [product for product in waiting if can_run(product)]
                     if runnable:
-                        multiply(min(runnable, key=age) if step < BY_AGE else runnable[0], step)
+                        multiply(min(runnable, key=age) if step < HEAD else runnable[0], step)
             if due:
-                drained.add(due[0])
+                parked[due[0]] = sums
 
-        for i in range(GPSIMD_TILES, tiles):
-            add_and_store(parked[i], 0, i, 1, nc.vector)
-        for i in range(tiles):
+        for i in range(TILES):
+            add_and_store(parked[i], 0, i, 1)
+        for i in range(TILES):
             for product in [product for product in waiting if product[2] == i]:
-                multiply(product, chunks)
-            add_and_store(acc[1, i], 1, i, 2 if i == tiles - 1 else 1, nc.vector)
+                multiply(product, CHUNKS)
+            add_and_store(acc[1, i], 1, i, 2 if i == TILES - 1 else 1)
         assert not waiting

@@ -24,6 +24,7 @@ RUN = 2
 
 SLABS = [("x", 0, 0), ("w", 0, 0), ("x", 1, 0), ("w", 1, 0), ("x", 0, 1), ("x", 1, 1)]
 CHUNKS = PER_SLAB * len(SLABS)
+PAIR = 2
 HEAD = 2 * PER_SLAB
 LEAD = BACK_BANKS - 1
 ROUND_LEAD = 3
@@ -39,19 +40,20 @@ def tile_mix_tierb_four_res_kernel(tc, w, x, res, out):
         ps = ctx.enter_context(tc.psum_pool(name="ps", bufs=1))
         ctx.enter_context(tc.manual_schedule())
 
-        groups = [(c, 1) for c in range(HEAD)] + [(c, 2) for c in range(HEAD, CHUNKS, 2)]
+        groups = [(c, 1) for c in range(HEAD)] + [(c, PAIR) for c in range(HEAD, CHUNKS, PAIR)]
+        vector_rounds = range(0, PER_SLAB, PAIR)
 
         raw = {}
-        for first, count in [(0, 2)] + groups[2:]:
+        for first in range(0, CHUNKS, PAIR):
             kind, g, h = SLABS[first // PER_SLAB]
             src = x if kind == "x" else w
-            piece = sb.tile([P, PACK, count * CHUNK], F32, name="raw%d" % first, align_bytes=64)
+            piece = sb.tile([P, PACK, PAIR * CHUNK], F32, name="raw%d" % first, align_bytes=64)
             col = h * WIDE + (first % PER_SLAB) * CHUNK
             nc.sync.dma_start(
                 out=piece[:],
-                in_=src[g * K_PASS : (g + 1) * K_PASS, col : col + count * CHUNK].rearrange("(p j) c -> p j c", j=PACK),
+                in_=src[g * K_PASS : (g + 1) * K_PASS, col : col + PAIR * CHUNK].rearrange("(p j) c -> p j c", j=PACK),
             )
-            for i in range(count):
+            for i in range(PAIR):
                 raw[first + i] = (piece, i * CHUNK)
         res_sb = {}
         for h in range(T // WIDE):
@@ -221,22 +223,23 @@ def tile_mix_tierb_four_res_kernel(tc, w, x, res, out):
                     out=out[i * P : (i + 1) * P, h * WIDE + lo : h * WIDE + lo + width], in_=result[:]
                 )
 
+        stored = 0
         for step in range(-LEAD - ROUND_LEAD, CHUNKS + 1):
-            for first, count in groups[1:]:
-                if first - LEAD - ROUND_LEAD == step:
+            for first, count in groups:
+                if first - LEAD - ROUND_LEAD == step and first not in vector_rounds:
                     nc.scalar.copy(out=interleaved("q", first, count), in_=raw_rows(first, count))
-            if step == -LEAD:
-                nc.vector.tensor_copy(out=interleaved("q", 0, 1), in_=raw_rows(0, 1))
             if 0 <= step < CHUNKS:
                 subtract(step)
             ahead = [group for group in groups if group[0] - LEAD == step]
             for group in ahead:
+                if group[0] in vector_rounds:
+                    nc.vector.tensor_copy(out=interleaved("q", *group), in_=raw_rows(*group))
                 quantise("q", *group)
             if step >= 1 and SLABS[(step - 1) // PER_SLAB][0] == "w":
                 quantise("r", step - 1, 1)
             if 0 <= step < CHUNKS and SLABS[step // PER_SLAB][0] == "x" and step % PER_SLAB == PER_SLAB - 1:
-                quantise("r", step - 3, 2)
-                quantise("r", step - 1, 2)
+                quantise("r", step + 1 - PER_SLAB, PAIR)
+                quantise("r", step + 1 - PAIR, PAIR)
             for group in ahead:
                 bring_back(*group)
             due = [i for h, i in closed_at if h == 0 and i not in parked and closed_at[h, i] + DRAIN_DELAY <= step]
@@ -244,6 +247,9 @@ def tile_mix_tierb_four_res_kernel(tc, w, x, res, out):
             if due:
                 sums = sb.tile([P, WIDE], F32, name="parked%d" % due[0])
                 nc.scalar.copy(out=sums[:], in_=acc[0, due[0]][:])
+            if CHUNKS - PER_SLAB <= step < CHUNKS and step % PAIR == 0:
+                add_and_store(parked[stored], 0, stored, 1)
+                stored = stored + 1
             if step < CHUNKS:
                 for slot in range(PRODUCTS_PER_STEP):
                     runnable = [product for product in waiting if can_run(product)]
@@ -252,7 +258,7 @@ def tile_mix_tierb_four_res_kernel(tc, w, x, res, out):
             if due:
                 parked[due[0]] = sums
 
-        for i in range(TILES):
+        for i in range(stored, TILES):
             add_and_store(parked[i], 0, i, 1)
         for i in range(TILES):
             for product in [product for product in waiting if product[2] == i]:

@@ -30,7 +30,6 @@ LEAD = BACK_BANKS - 1
 ROUND_LEAD = 3
 PRODUCTS_PER_STEP = 3
 DRAIN_DELAY = 2
-WARM_UP_PASSES = 10
 
 
 def tile_mix_tierb_four_res_kernel(tc, w, x, res, out):
@@ -86,24 +85,10 @@ def tile_mix_tierb_four_res_kernel(tc, w, x, res, out):
                 in_=eye[:, lo * K_PASS : hi * K_PASS],
             )
 
-        mark(0)
-        mark(1)
-        quantise_eye(0, 1)
-        mark(2)
-        mark(3)
-        quantise_eye(1, 2)
+        for j in range(PACK):
+            mark(j)
+        quantise_eye(0, 2)
         quantise_eye(2, 4)
-        idle = ps.tile([P, CHUNK], F32, name="idle", tag="acc%d" % (TILES - 1))
-        for i in range(WARM_UP_PASSES):
-            nc.tensor.matmul_mx(
-                out=idle[:],
-                lhsT=eye_codes[:, 0:P].bitcast(FORMAT["q"]),
-                lhsT_scale=eye_scales[:, 0:P],
-                rhs=eye_codes[:, 0:P].bitcast(FORMAT["q"]),
-                rhs_scale=eye_scales[:, 0:P],
-                start=True,
-                stop=True,
-            )
 
         rounded = {}
         codes = {}

@@ -29,6 +29,8 @@ HEAD = 2 * PER_SLAB
 LEAD = BACK_BANKS - 1
 ROUND_LEAD = 3
 PRODUCTS_PER_STEP = 3
+WIDE_PAIRS = (8, 16, 18, 20, 22)
+LATE = 2
 DRAIN_DELAY = 2
 
 
@@ -121,8 +123,27 @@ def tile_mix_tierb_four_res_kernel(tc, w, x, res, out):
                 made[tier, c] = len(made)
 
         back = {}
+        halves = {}
 
         def bring_back(first, count):
+            if first in WIDE_PAIRS:
+                s, lo = first // PER_SLAB, (first % PER_SLAB) * CHUNK
+                for j in range(PACK):
+                    c = first + j // 2
+                    if j % 2 == 0:
+                        back[c] = ps.tile(
+                            [P, 2, PAIR * CHUNK], F32, name="back%d" % c, tag="back%d" % (c % BACK_BANKS)
+                        )
+                    nc.tensor.matmul_mx(
+                        out=back[c][:, j % 2, :],
+                        lhsT=eye_codes[:, j * P : (j + 1) * P].bitcast(FORMAT["q"]),
+                        lhsT_scale=eye_scales[:, j * P : (j + 1) * P],
+                        rhs=codes["q", s][:, lo : lo + PAIR * CHUNK].bitcast(FORMAT["q"]),
+                        rhs_scale=scales["q", s][:, lo : lo + PAIR * CHUNK],
+                        start=True,
+                        stop=True,
+                    )
+                return
             for c in range(first, first + count):
                 back[c] = ps.tile([P, PACK, CHUNK], F32, name="back%d" % c, tag="back%d" % (c % BACK_BANKS))
             for j in range(PACK):
@@ -139,6 +160,25 @@ def tile_mix_tierb_four_res_kernel(tc, w, x, res, out):
                     )
 
         def subtract(c):
+            first, u = c - c % PAIR, c % PAIR
+            if first in WIDE_PAIRS:
+                if u == 0:
+                    halves[first] = sb.tile([P, 2 * 2 * PAIR * CHUNK], BF16, name="halves%d" % first, align_bytes=64)
+                width = 2 * PAIR * CHUNK
+                nc.vector.tensor_tensor(
+                    out=halves[first][:, u * width : (u + 1) * width].rearrange("p (c i e) -> p c e i", i=4, e=2),
+                    in0=raw[first][0][:, 2 * u : 2 * u + 2, :].rearrange("p e (c i) -> p c e i", i=4),
+                    in1=back[c][:].rearrange("p e (c i) -> p c e i", i=4),
+                    op=mybir.AluOpType.subtract,
+                )
+                if u == 1:
+                    lo = (first % PER_SLAB) * CHUNK * PACK
+                    flat = rounded["r", first // PER_SLAB][:, lo : lo + PAIR * CHUNK * PACK]
+                    nc.scalar.copy(
+                        out=flat.bitcast(U32).rearrange("p (c i u) -> p c u i", i=RUN, u=2),
+                        in_=halves[first][:].bitcast(U32).rearrange("p (u c i) -> p c u i", i=RUN, u=2),
+                    )
+                return
             nc.vector.tensor_tensor(
                 out=interleaved("r", c, 1),
                 in0=raw_rows(c, 1),
@@ -220,11 +260,16 @@ def tile_mix_tierb_four_res_kernel(tc, w, x, res, out):
                 if group[0] in vector_rounds:
                     nc.vector.tensor_copy(out=interleaved("q", *group), in_=raw_rows(*group))
                 quantise("q", *group)
-            if step >= 1 and SLABS[(step - 1) // PER_SLAB][0] == "w":
+            if step >= 1 and SLABS[(step - 1) // PER_SLAB][0] == "w" and (step - 1) // PAIR * PAIR not in WIDE_PAIRS:
                 quantise("r", step - 1, 1)
             if 0 <= step < CHUNKS and SLABS[step // PER_SLAB][0] == "x" and step % PER_SLAB == PER_SLAB - 1:
                 quantise("r", step + 1 - PER_SLAB, PAIR)
-                quantise("r", step + 1 - PAIR, PAIR)
+                if step - 1 not in WIDE_PAIRS:
+                    quantise("r", step + 1 - PAIR, PAIR)
+            for first in WIDE_PAIRS:
+                late = min(first + 1 + LATE, CHUNKS)
+                if step == late and (SLABS[first // PER_SLAB][0] == "w" or first % PER_SLAB == PAIR):
+                    quantise("r", first, PAIR)
             for group in ahead:
                 bring_back(*group)
             due = [i for h, i in closed_at if h == 0 and i not in parked and closed_at[h, i] + DRAIN_DELAY <= step]

@@ -14,13 +14,15 @@ FORMAT = {"q": mybir.dt.float8_e4m3fn_x4, "r": mybir.dt.float8_e5m2_x4}
 P = 128
 PACK = 4
 K_PASS = P * PACK
-WIDE = 512
+SLAB_COLS = 512
 CHUNK = 128
-PER_SLAB = WIDE // CHUNK
+PER_SLAB = SLAB_COLS // CHUNK
 TILES = N // P
 BACK_BANKS = 8 - TILES
 PASSES_PER_TILE = 4 * (K // K_PASS)
 RUN = 2
+HALF = PACK // 2
+HALF_RUN = 4
 
 SLABS = [("x", 0, 0), ("w", 0, 0), ("x", 1, 0), ("w", 1, 0), ("x", 0, 1), ("x", 1, 1)]
 CHUNKS = PER_SLAB * len(SLABS)
@@ -29,9 +31,8 @@ HEAD = 2 * PER_SLAB
 LEAD = BACK_BANKS - 1
 ROUND_LEAD = 3
 PRODUCTS_PER_STEP = 3
-WIDE_PAIRS = (8, 16, 18, 20, 22)
-LATE = 2
 DRAIN_DELAY = 2
+JOIN_DELAY = 2
 
 
 def tile_mix_tierb_four_res_kernel(tc, w, x, res, out):
@@ -42,6 +43,8 @@ def tile_mix_tierb_four_res_kernel(tc, w, x, res, out):
         ctx.enter_context(tc.manual_schedule())
 
         groups = [(c, 1) for c in range(HEAD)] + [(c, PAIR) for c in range(HEAD, CHUNKS, PAIR)]
+        awaited = PER_SLAB * SLABS.index(("x", 1, 0)) + PAIR
+        wide_pairs = [c for c in range(HEAD, CHUNKS, PAIR) if SLABS[c // PER_SLAB][0] == "x" and c != awaited]
         vector_rounds = range(0, PER_SLAB, PAIR)
 
         raw = {}
@@ -49,7 +52,7 @@ def tile_mix_tierb_four_res_kernel(tc, w, x, res, out):
             kind, g, h = SLABS[first // PER_SLAB]
             src = x if kind == "x" else w
             piece = sb.tile([P, PACK, PAIR * CHUNK], F32, name="raw%d" % first, align_bytes=64)
-            col = h * WIDE + (first % PER_SLAB) * CHUNK
+            col = h * SLAB_COLS + (first % PER_SLAB) * CHUNK
             nc.sync.dma_start(
                 out=piece[:],
                 in_=src[g * K_PASS : (g + 1) * K_PASS, col : col + PAIR * CHUNK].rearrange("(p j) c -> p j c", j=PACK),
@@ -57,10 +60,10 @@ def tile_mix_tierb_four_res_kernel(tc, w, x, res, out):
             for i in range(PAIR):
                 raw[first + i] = (piece, i * CHUNK)
         res_sb = {}
-        for h in range(T // WIDE):
-            res_sb[h] = sb.tile([P, TILES, WIDE], F32, name="res%d" % h)
+        for h in range(T // SLAB_COLS):
+            res_sb[h] = sb.tile([P, TILES, SLAB_COLS], F32, name="res%d" % h)
             nc.sync.dma_start(
-                out=res_sb[h][:], in_=res[:, h * WIDE : (h + 1) * WIDE].rearrange("(i p) t -> p i t", p=P)
+                out=res_sb[h][:], in_=res[:, h * SLAB_COLS : (h + 1) * SLAB_COLS].rearrange("(i p) t -> p i t", p=P)
             )
 
         ramp = sb.tile([P, K_PASS], BF16, name="ramp", align_bytes=64)
@@ -89,17 +92,16 @@ def tile_mix_tierb_four_res_kernel(tc, w, x, res, out):
 
         for j in range(PACK):
             mark(j)
-        quantise_eye(0, 2)
-        quantise_eye(2, 4)
+        quantise_eye(0, HALF)
 
         rounded = {}
         codes = {}
         scales = {}
         for s in range(len(SLABS)):
             for tier in "qr":
-                rounded[tier, s] = sb.tile([P, WIDE * PACK], BF16, name="rounded_%s%d" % (tier, s), align_bytes=256)
-                codes[tier, s] = sb.tile([P, WIDE], U32, name="codes_%s%d" % (tier, s), align_bytes=256)
-                scales[tier, s] = sb.tile([P, WIDE], U8, name="scales_%s%d" % (tier, s), align_bytes=256)
+                rounded[tier, s] = sb.tile([P, SLAB_COLS * PACK], BF16, name="rounded_%s%d" % (tier, s), align_bytes=256)
+                codes[tier, s] = sb.tile([P, SLAB_COLS], U32, name="codes_%s%d" % (tier, s), align_bytes=256)
+                scales[tier, s] = sb.tile([P, SLAB_COLS], U8, name="scales_%s%d" % (tier, s), align_bytes=256)
 
         def interleaved(tier, first, count):
             lo = (first % PER_SLAB) * CHUNK * PACK
@@ -123,67 +125,56 @@ def tile_mix_tierb_four_res_kernel(tc, w, x, res, out):
                 made[tier, c] = len(made)
 
         back = {}
-        halves = {}
+        words = {}
+
+        def pass_back(target, j, first, count):
+            s, lo = first // PER_SLAB, (first % PER_SLAB) * CHUNK
+            nc.tensor.matmul_mx(
+                out=target,
+                lhsT=eye_codes[:, j * P : (j + 1) * P].bitcast(FORMAT["q"]),
+                lhsT_scale=eye_scales[:, j * P : (j + 1) * P],
+                rhs=codes["q", s][:, lo : lo + count * CHUNK].bitcast(FORMAT["q"]),
+                rhs_scale=scales["q", s][:, lo : lo + count * CHUNK],
+                start=True,
+                stop=True,
+            )
 
         def bring_back(first, count):
-            if first in WIDE_PAIRS:
-                s, lo = first // PER_SLAB, (first % PER_SLAB) * CHUNK
-                for j in range(PACK):
-                    c = first + j // 2
-                    if j % 2 == 0:
-                        back[c] = ps.tile(
-                            [P, 2, PAIR * CHUNK], F32, name="back%d" % c, tag="back%d" % (c % BACK_BANKS)
-                        )
-                    nc.tensor.matmul_mx(
-                        out=back[c][:, j % 2, :],
-                        lhsT=eye_codes[:, j * P : (j + 1) * P].bitcast(FORMAT["q"]),
-                        lhsT_scale=eye_scales[:, j * P : (j + 1) * P],
-                        rhs=codes["q", s][:, lo : lo + PAIR * CHUNK].bitcast(FORMAT["q"]),
-                        rhs_scale=scales["q", s][:, lo : lo + PAIR * CHUNK],
-                        start=True,
-                        stop=True,
-                    )
-                return
+            shape = [P, HALF, PAIR * CHUNK] if first in wide_pairs else [P, PACK, CHUNK]
             for c in range(first, first + count):
-                back[c] = ps.tile([P, PACK, CHUNK], F32, name="back%d" % c, tag="back%d" % (c % BACK_BANKS))
+                back[c] = ps.tile(shape, F32, name="back%d" % c, tag="back%d" % (c % BACK_BANKS))
             for j in range(PACK):
-                for c in range(first, first + count):
-                    s, lo = c // PER_SLAB, (c % PER_SLAB) * CHUNK
-                    nc.tensor.matmul_mx(
-                        out=back[c][:, j, :],
-                        lhsT=eye_codes[:, j * P : (j + 1) * P].bitcast(FORMAT["q"]),
-                        lhsT_scale=eye_scales[:, j * P : (j + 1) * P],
-                        rhs=codes["q", s][:, lo : lo + CHUNK].bitcast(FORMAT["q"]),
-                        rhs_scale=scales["q", s][:, lo : lo + CHUNK],
-                        start=True,
-                        stop=True,
-                    )
+                if first in wide_pairs:
+                    pass_back(back[first + j // HALF][:, j % HALF, :], j, first, PAIR)
+                else:
+                    for c in range(first, first + count):
+                        pass_back(back[c][:, j, :], j, c, 1)
 
-        def subtract(c):
-            first, u = c - c % PAIR, c % PAIR
-            if first in WIDE_PAIRS:
-                if u == 0:
-                    halves[first] = sb.tile([P, 2 * 2 * PAIR * CHUNK], BF16, name="halves%d" % first, align_bytes=64)
-                width = 2 * PAIR * CHUNK
-                nc.vector.tensor_tensor(
-                    out=halves[first][:, u * width : (u + 1) * width].rearrange("p (c i e) -> p c e i", i=4, e=2),
-                    in0=raw[first][0][:, 2 * u : 2 * u + 2, :].rearrange("p e (c i) -> p c e i", i=4),
-                    in1=back[c][:].rearrange("p e (c i) -> p c e i", i=4),
-                    op=mybir.AluOpType.subtract,
-                )
-                if u == 1:
-                    lo = (first % PER_SLAB) * CHUNK * PACK
-                    flat = rounded["r", first // PER_SLAB][:, lo : lo + PAIR * CHUNK * PACK]
-                    nc.scalar.copy(
-                        out=flat.bitcast(U32).rearrange("p (c i u) -> p c u i", i=RUN, u=2),
-                        in_=halves[first][:].bitcast(U32).rearrange("p (u c i) -> p c u i", i=RUN, u=2),
-                    )
-                return
+        def subtract_narrow(c):
             nc.vector.tensor_tensor(
                 out=interleaved("r", c, 1),
                 in0=raw_rows(c, 1),
                 in1=back[c][:].rearrange("p j (c i) -> p c j i", i=RUN),
                 op=mybir.AluOpType.subtract,
+            )
+
+        def subtract_wide(first, u):
+            width = HALF * PAIR * CHUNK
+            if u == 0:
+                words[first] = sb.tile([P, 2 * width], BF16, name="words%d" % first, align_bytes=64)
+            nc.vector.tensor_tensor(
+                out=words[first][:, u * width : (u + 1) * width].rearrange("p (c i e) -> p c e i", i=HALF_RUN, e=HALF),
+                in0=raw[first][0][:, HALF * u : HALF * (u + 1), :].rearrange("p e (c i) -> p c e i", i=HALF_RUN),
+                in1=back[first + u][:].rearrange("p e (c i) -> p c e i", i=HALF_RUN),
+                op=mybir.AluOpType.subtract,
+            )
+
+        def join_words(first):
+            lo = (first % PER_SLAB) * CHUNK * PACK
+            flat = rounded["r", first // PER_SLAB][:, lo : lo + PAIR * CHUNK * PACK]
+            nc.scalar.copy(
+                out=flat.bitcast(U32).rearrange("p (c i u) -> p c u i", i=RUN, u=2),
+                in_=words[first][:].bitcast(U32).rearrange("p (u c i) -> p c u i", i=RUN, u=2),
             )
 
         acc = {}
@@ -192,7 +183,7 @@ def tile_mix_tierb_four_res_kernel(tc, w, x, res, out):
         parked = {}
         waiting = [
             (h, g, i, w_tier, x_tier)
-            for h in range(T // WIDE)
+            for h in range(T // SLAB_COLS)
             for g in range(K // K_PASS)
             for i in range(TILES)
             for w_tier in "qr"
@@ -217,7 +208,7 @@ def tile_mix_tierb_four_res_kernel(tc, w, x, res, out):
             xs, ws = SLABS.index(("x", g, h)), SLABS.index(("w", g, 0))
             done = passes_done.get((h, i), 0)
             if done == 0:
-                acc[h, i] = ps.tile([P, WIDE], F32, name="acc%d_%d" % (h, i), tag="acc%d" % i)
+                acc[h, i] = ps.tile([P, SLAB_COLS], F32, name="acc%d_%d" % (h, i), tag="acc%d" % i)
             nc.tensor.matmul_mx(
                 out=acc[h, i][:],
                 lhsT=codes[w_tier, ws][:, i * P : (i + 1) * P].bitcast(FORMAT[w_tier]),
@@ -233,7 +224,7 @@ def tile_mix_tierb_four_res_kernel(tc, w, x, res, out):
             waiting.remove(product)
 
         def add_and_store(sums, h, i, parts):
-            width = WIDE // parts
+            width = SLAB_COLS // parts
             for part in range(parts):
                 lo = part * width
                 result = sb.tile([P, width], F32, name="result%d_%d_%d" % (h, i, part))
@@ -245,7 +236,7 @@ def tile_mix_tierb_four_res_kernel(tc, w, x, res, out):
                 )
                 queue = nc.sync if part == 0 else nc.scalar
                 queue.dma_start(
-                    out=out[i * P : (i + 1) * P, h * WIDE + lo : h * WIDE + lo + width], in_=result[:]
+                    out=out[i * P : (i + 1) * P, h * SLAB_COLS + lo : h * SLAB_COLS + lo + width], in_=result[:]
                 )
 
         stored = 0
@@ -253,35 +244,41 @@ def tile_mix_tierb_four_res_kernel(tc, w, x, res, out):
             for first, count in groups:
                 if first - LEAD - ROUND_LEAD == step and first not in vector_rounds:
                     nc.scalar.copy(out=interleaved("q", first, count), in_=raw_rows(first, count))
-            if 0 <= step < CHUNKS:
-                subtract(step)
+            pair, u = step - step % PAIR, step % PAIR
+            if pair in wide_pairs:
+                subtract_wide(pair, u)
+                if u == 1:
+                    join_words(pair)
+            elif 0 <= step < CHUNKS:
+                subtract_narrow(step)
             ahead = [group for group in groups if group[0] - LEAD == step]
             for group in ahead:
                 if group[0] in vector_rounds:
                     nc.vector.tensor_copy(out=interleaved("q", *group), in_=raw_rows(*group))
+                if group[0] == 0:
+                    quantise_eye(HALF, PACK)
                 quantise("q", *group)
-            if step >= 1 and SLABS[(step - 1) // PER_SLAB][0] == "w" and (step - 1) // PAIR * PAIR not in WIDE_PAIRS:
+            if step >= 1 and SLABS[(step - 1) // PER_SLAB][0] == "w":
                 quantise("r", step - 1, 1)
             if 0 <= step < CHUNKS and SLABS[step // PER_SLAB][0] == "x" and step % PER_SLAB == PER_SLAB - 1:
-                quantise("r", step + 1 - PER_SLAB, PAIR)
-                if step - 1 not in WIDE_PAIRS:
-                    quantise("r", step + 1 - PAIR, PAIR)
-            for first in WIDE_PAIRS:
-                late = min(first + 1 + LATE, CHUNKS)
-                if step == late and (SLABS[first // PER_SLAB][0] == "w" or first % PER_SLAB == PAIR):
+                quantise("r", pair - PAIR, PAIR)
+                if pair not in wide_pairs:
+                    quantise("r", pair, PAIR)
+            for first in wide_pairs:
+                if first % PER_SLAB == PAIR and step == min(first + 1 + JOIN_DELAY, CHUNKS):
                     quantise("r", first, PAIR)
             for group in ahead:
                 bring_back(*group)
             due = [i for h, i in closed_at if h == 0 and i not in parked and closed_at[h, i] + DRAIN_DELAY <= step]
             sums = None
             if due:
-                sums = sb.tile([P, WIDE], F32, name="parked%d" % due[0])
+                sums = sb.tile([P, SLAB_COLS], F32, name="parked%d" % due[0])
                 nc.scalar.copy(out=sums[:], in_=acc[0, due[0]][:])
             if CHUNKS - PER_SLAB <= step < CHUNKS and step % PAIR == 0:
                 add_and_store(parked[stored], 0, stored, 1)
                 stored = stored + 1
             if step < CHUNKS:
-                for slot in range(PRODUCTS_PER_STEP):
+                for slot in range(PRODUCTS_PER_STEP + 1 if step < HEAD else PRODUCTS_PER_STEP):
                     runnable = [product for product in waiting if can_run(product)]
                     if runnable:
                         multiply(min(runnable, key=age) if step < HEAD else runnable[0], step)

@@ -234,8 +234,7 @@ def tile_mix_tierb_four_res_kernel(tc, w, x, res, out):
                     in1=sums[:, lo : lo + width],
                     op=mybir.AluOpType.add,
                 )
-                queue = nc.sync if part == 0 else nc.scalar
-                queue.dma_start(
+                nc.sync.dma_start(
                     out=out[i * P : (i + 1) * P, h * SLAB_COLS + lo : h * SLAB_COLS + lo + width], in_=result[:]
                 )
 
@@ -264,6 +263,9 @@ def tile_mix_tierb_four_res_kernel(tc, w, x, res, out):
                 quantise("r", pair - PAIR, PAIR)
                 if pair not in wide_pairs:
                     quantise("r", pair, PAIR)
+            if step == CHUNKS:
+                add_and_store(parked[stored], 0, stored, 1)
+                stored = stored + 1
             for first in wide_pairs:
                 if first % PER_SLAB == PAIR and step == min(first + 1 + JOIN_DELAY, CHUNKS):
                     quantise("r", first, PAIR)

@@ -45,6 +45,7 @@ def tile_mix_tierb_four_res_kernel(tc, w, x, res, out):
         groups = [(c, 1) for c in range(HEAD)] + [(c, PAIR) for c in range(HEAD, CHUNKS, PAIR)]
         awaited = PER_SLAB * SLABS.index(("x", 1, 0)) + PAIR
         wide_pairs = [c for c in range(HEAD, CHUNKS, PAIR) if SLABS[c // PER_SLAB][0] == "x" and c != awaited]
+        last_w = PER_SLAB * SLABS.index(("w", 1, 0)) + PAIR
         vector_rounds = range(0, PER_SLAB, PAIR)
 
         raw = {}
@@ -241,9 +242,14 @@ def tile_mix_tierb_four_res_kernel(tc, w, x, res, out):
         stored = 0
         for step in range(-LEAD - ROUND_LEAD, CHUNKS + 1):
             for first, count in groups:
-                if first - LEAD - ROUND_LEAD == step and first not in vector_rounds:
+                lead = LEAD + ROUND_LEAD + (PAIR if first == CHUNKS - PAIR else 0)
+                if first - lead == step and first not in vector_rounds:
                     nc.scalar.copy(out=interleaved("q", first, count), in_=raw_rows(first, count))
             pair, u = step - step % PAIR, step % PAIR
+            if step == last_w - LEAD:
+                quantise("q", last_w, PAIR)
+                for i in range(TILES - PAIR, TILES):
+                    multiply((0, 1, i, "q", "q"), step)
             if pair in wide_pairs:
                 subtract_wide(pair, u)
                 if u == 1:
@@ -256,7 +262,8 @@ def tile_mix_tierb_four_res_kernel(tc, w, x, res, out):
                     nc.vector.tensor_copy(out=interleaved("q", *group), in_=raw_rows(*group))
                 if group[0] == 0:
                     quantise_eye(HALF, PACK)
-                quantise("q", *group)
+                if group[0] != last_w:
+                    quantise("q", *group)
             if step >= 1 and SLABS[(step - 1) // PER_SLAB][0] == "w":
                 quantise("r", step - 1, 1)
             if 0 <= step < CHUNKS and SLABS[step // PER_SLAB][0] == "x" and step % PER_SLAB == PER_SLAB - 1:

@@ -191,6 +191,8 @@ def tile_mix_tierb_four_res_kernel(tc, w, x, res, out):
             for x_tier in "qr"
         ]
 
+        last_tile = [product for product in waiting if (product[0], product[2]) == (1, TILES - 1)]
+
         def operands(product):
             h, g, i, w_tier, x_tier = product
             w_chunk = PER_SLAB * SLABS.index(("w", g, 0)) + i
@@ -204,40 +206,42 @@ def tile_mix_tierb_four_res_kernel(tc, w, x, res, out):
         def age(product):
             return max(made[operand] for operand in operands(product))
 
-        def multiply(product, step):
+        def multiply(product, step, lo=0, cols=SLAB_COLS // 2):
             h, g, i, w_tier, x_tier = product
             xs, ws = SLABS.index(("x", g, h)), SLABS.index(("w", g, 0))
-            done = passes_done.get((h, i), 0)
+            cols = cols if product in last_tile else SLAB_COLS
+            tile = (h, i, lo) if lo else (h, i)
+            done = passes_done.get(tile, 0)
             if done == 0:
-                acc[h, i] = ps.tile([P, SLAB_COLS], F32, name="acc%d_%d" % (h, i), tag="acc%d" % i)
+                acc[tile] = ps.tile([P, SLAB_COLS], F32, name="acc%d_%d_%d" % (h, i, lo), tag="back%d" % (lo // CHUNK - 2) if lo else "acc%d" % i)
             nc.tensor.matmul_mx(
-                out=acc[h, i][:],
+                out=acc[tile][:, lo : lo + cols],
                 lhsT=codes[w_tier, ws][:, i * P : (i + 1) * P].bitcast(FORMAT[w_tier]),
                 lhsT_scale=scales[w_tier, ws][:, i * P : (i + 1) * P],
-                rhs=codes[x_tier, xs][:].bitcast(FORMAT[x_tier]),
-                rhs_scale=scales[x_tier, xs][:],
+                rhs=codes[x_tier, xs][:, lo : lo + cols].bitcast(FORMAT[x_tier]),
+                rhs_scale=scales[x_tier, xs][:, lo : lo + cols],
                 start=done == 0,
                 stop=done == PASSES_PER_TILE - 1,
             )
-            passes_done[h, i] = done + 1
-            if done == PASSES_PER_TILE - 1:
-                closed_at[h, i] = step
-            waiting.remove(product)
+            passes_done[tile] = done + 1
+            if not lo:
+                if done == PASSES_PER_TILE - 1:
+                    closed_at[h, i] = step
+                waiting.remove(product)
 
-        def add_and_store(sums, h, i, parts):
+        def add_and_store(sums, h, i, parts, part=0):
             width = SLAB_COLS // parts
-            for part in range(parts):
-                lo = part * width
-                result = sb.tile([P, width], F32, name="result%d_%d_%d" % (h, i, part))
-                nc.vector.tensor_tensor(
-                    out=result[:],
-                    in0=res_sb[h][:, i, lo : lo + width],
-                    in1=sums[:, lo : lo + width],
-                    op=mybir.AluOpType.add,
-                )
-                nc.sync.dma_start(
-                    out=out[i * P : (i + 1) * P, h * SLAB_COLS + lo : h * SLAB_COLS + lo + width], in_=result[:]
-                )
+            lo = part * width
+            result = sb.tile([P, width], F32, name="result%d_%d_%d" % (h, i, part))
+            nc.vector.tensor_tensor(
+                out=result[:],
+                in0=res_sb[h][:, i, lo : lo + width],
+                in1=sums[:, lo : lo + width],
+                op=mybir.AluOpType.add,
+            )
+            nc.sync.dma_start(
+                out=out[i * P : (i + 1) * P, h * SLAB_COLS + lo : h * SLAB_COLS + lo + width], in_=result[:]
+            )
 
         stored = 0
         for step in range(-LEAD - ROUND_LEAD, CHUNKS + 1):
@@ -283,7 +287,7 @@ def tile_mix_tierb_four_res_kernel(tc, w, x, res, out):
             if due:
                 sums = sb.tile([P, SLAB_COLS], F32, name="parked%d" % due[0])
                 nc.scalar.copy(out=sums[:], in_=acc[0, due[0]][:])
-            if CHUNKS - PER_SLAB <= step < CHUNKS and step % PAIR == 0:
+            if step == CHUNKS - PER_SLAB:
                 add_and_store(parked[stored], 0, stored, 1)
                 stored = stored + 1
             if step < CHUNKS:
@@ -300,4 +304,8 @@ def tile_mix_tierb_four_res_kernel(tc, w, x, res, out):
             for product in [product for product in waiting if product[2] == i]:
                 multiply(product, CHUNKS)
             add_and_store(acc[1, i], 1, i, 2 if i == TILES - 1 else 1)
+        for part in range(2, PER_SLAB):
+            for product in last_tile:
+                multiply(product, CHUNKS, part * CHUNK, CHUNK)
+            add_and_store(acc[1, TILES - 1, part * CHUNK], 1, TILES - 1, PER_SLAB, part)
         assert not waiting

@@ -14,25 +14,19 @@ FORMAT = {"q": mybir.dt.float8_e4m3fn_x4, "r": mybir.dt.float8_e5m2_x4}
 P = 128
 PACK = 4
 K_PASS = P * PACK
-SLAB_COLS = 512
+BANK = 512
 CHUNK = 128
-PER_SLAB = SLAB_COLS // CHUNK
+PAIR = 2
 TILES = N // P
-BACK_BANKS = 8 - TILES
-PASSES_PER_TILE = 4 * (K // K_PASS)
+BACK_BANKS = 4
 RUN = 2
 HALF = PACK // 2
 HALF_RUN = 4
 
-SLABS = [("x", 0, 0), ("w", 0, 0), ("x", 1, 0), ("w", 1, 0), ("x", 0, 1), ("x", 1, 1)]
-CHUNKS = PER_SLAB * len(SLABS)
-PAIR = 2
-HEAD = 2 * PER_SLAB
-LEAD = BACK_BANKS - 1
-ROUND_LEAD = 3
-PRODUCTS_PER_STEP = 3
-DRAIN_DELAY = 2
-JOIN_DELAY = 2
+LOADS = [(kind, g, c, 2) for g in range(2) for kind in "xw" for c in (0, 2)] + [("x", g, c, 2) for g in range(2) for c in (4, 6)] + [("res", 0, i, 0) for i in range(4)]
+HEAD = 8
+BANK_OF = {}
+WIDE = [8, 16, 18, 20, 22]
 
 
 def tile_mix_tierb_four_res_kernel(tc, w, x, res, out):
@@ -42,111 +36,110 @@ def tile_mix_tierb_four_res_kernel(tc, w, x, res, out):
         ps = ctx.enter_context(tc.psum_pool(name="ps", bufs=1))
         ctx.enter_context(tc.manual_schedule())
 
-        groups = [(c, 1) for c in range(HEAD)] + [(c, PAIR) for c in range(HEAD, CHUNKS, PAIR)]
-        awaited = PER_SLAB * SLABS.index(("x", 1, 0)) + PAIR
-        wide_pairs = [c for c in range(HEAD, CHUNKS, PAIR) if SLABS[c // PER_SLAB][0] == "x" and c != awaited]
-        last_w = PER_SLAB * SLABS.index(("w", 1, 0)) + PAIR
-        vector_rounds = range(0, PER_SLAB, PAIR)
-
-        raw = {}
-        for first in range(0, CHUNKS, PAIR):
-            kind, g, h = SLABS[first // PER_SLAB]
+        chunks = []
+        raw = []
+        res_sb = {}
+        for kind, g, first, count in LOADS:
+            if kind == "res":
+                res_sb[first] = sb.tile([P, T], F32, name="res%d" % first)
+                nc.sync.dma_start(out=res_sb[first][:], in_=res[first * P : (first + 1) * P, :])
+                continue
             src = x if kind == "x" else w
-            piece = sb.tile([P, PACK, PAIR * CHUNK], F32, name="raw%d" % first, align_bytes=64)
-            col = h * SLAB_COLS + (first % PER_SLAB) * CHUNK
+            piece = sb.tile([P, PACK, count * CHUNK], F32, name="raw%d" % len(chunks), align_bytes=64)
             nc.sync.dma_start(
                 out=piece[:],
-                in_=src[g * K_PASS : (g + 1) * K_PASS, col : col + PAIR * CHUNK].rearrange("(p j) c -> p j c", j=PACK),
+                in_=src[g * K_PASS : (g + 1) * K_PASS, first * CHUNK : (first + count) * CHUNK].rearrange(
+                    "(p j) c -> p j c", j=PACK
+                ),
             )
-            for i in range(PAIR):
-                raw[first + i] = (piece, i * CHUNK)
-        res_sb = {}
-        for h in range(T // SLAB_COLS):
-            res_sb[h] = sb.tile([P, TILES, SLAB_COLS], F32, name="res%d" % h)
-            nc.sync.dma_start(
-                out=res_sb[h][:], in_=res[:, h * SLAB_COLS : (h + 1) * SLAB_COLS].rearrange("(i p) t -> p i t", p=P)
-            )
+            for i in range(count):
+                chunks.append((kind, g, first + i))
+                raw.append((piece, i * CHUNK))
+        last = len(chunks)
+        groups = [(c, 1) for c in range(HEAD)] + [(c, PAIR) for c in range(HEAD, last, PAIR)]
 
-        ramp = sb.tile([P, K_PASS], BF16, name="ramp", align_bytes=64)
-        nc.gpsimd.iota(
-            ramp[:], pattern=[[1, K_PASS]], base=0, channel_multiplier=-PACK, allow_small_or_imprecise_dtypes=True
-        )
         eye = sb.tile([P, PACK * K_PASS], BF16, name="eye", align_bytes=64)
         eye_codes = sb.tile([P, K_PASS], U32, name="eye_codes", align_bytes=256)
         eye_scales = sb.tile([P, K_PASS], U8, name="eye_scales", align_bytes=256)
-
-        def mark(j):
-            nc.vector.tensor_scalar(
-                out=eye[:, j * K_PASS : (j + 1) * K_PASS],
-                in0=ramp[:],
-                scalar1=float(j),
-                scalar2=None,
-                op0=mybir.AluOpType.is_equal,
-            )
-
-        def quantise_eye(lo, hi):
-            nc.vector.quantize_mx(
-                out=eye_codes[:, lo * P : hi * P].bitcast(FORMAT["q"]),
-                scales=eye_scales[:, lo * P : hi * P],
-                in_=eye[:, lo * K_PASS : hi * K_PASS],
-            )
-
+        ramp = sb.tile([P, P * HALF], BF16, name="ramp", align_bytes=64)
+        nc.gpsimd.iota(
+            ramp[:], pattern=[[1, P * HALF]], base=0, channel_multiplier=-HALF, allow_small_or_imprecise_dtypes=True
+        )
         for j in range(PACK):
-            mark(j)
-        quantise_eye(0, HALF)
+            nc.vector.tensor_scalar(
+                out=eye[:, j * K_PASS : (j + 1) * K_PASS].bitcast(mybir.dt.int32),
+                in0=ramp[:],
+                scalar1=float(j // HALF),
+                scalar2=float(0x3F80 << (16 * (j % HALF))),
+                op0=mybir.AluOpType.is_equal,
+                op1=mybir.AluOpType.mult,
+            )
+        for lo in range(0, PACK, HALF):
+            nc.vector.quantize_mx(
+                out=eye_codes[:, lo * P : (lo + HALF) * P].bitcast(FORMAT["q"]),
+                scales=eye_scales[:, lo * P : (lo + HALF) * P],
+                in_=eye[:, lo * K_PASS : (lo + HALF) * K_PASS],
+            )
 
         rounded = {}
         codes = {}
         scales = {}
-        for s in range(len(SLABS)):
-            for tier in "qr":
-                rounded[tier, s] = sb.tile([P, SLAB_COLS * PACK], BF16, name="rounded_%s%d" % (tier, s), align_bytes=256)
-                codes[tier, s] = sb.tile([P, SLAB_COLS], U32, name="codes_%s%d" % (tier, s), align_bytes=256)
-                scales[tier, s] = sb.tile([P, SLAB_COLS], U8, name="scales_%s%d" % (tier, s), align_bytes=256)
+        for kind, cols in (("x", T), ("w", N)):
+            for g in range(K // K_PASS):
+                for tier in "qr":
+                    label = "%s%s%d" % (kind, tier, g)
+                    rounded[tier, kind, g] = sb.tile([P, cols * PACK], BF16, name="rounded_" + label, align_bytes=256)
+                    codes[tier, kind, g] = sb.tile([P, cols], U32, name="codes_" + label, align_bytes=256)
+                    scales[tier, kind, g] = sb.tile([P, cols], U8, name="scales_" + label, align_bytes=256)
+
+        def flat(tier, first, count):
+            kind, g, col = chunks[first]
+            return rounded[tier, kind, g][:, col * CHUNK * PACK : (col + count) * CHUNK * PACK]
 
         def interleaved(tier, first, count):
-            lo = (first % PER_SLAB) * CHUNK * PACK
-            flat = rounded[tier, first // PER_SLAB][:, lo : lo + count * CHUNK * PACK]
-            return flat.rearrange("p (c i j) -> p c j i", i=RUN, j=PACK)
+            return flat(tier, first, count).rearrange("p (c i j) -> p c j i", i=RUN, j=PACK)
 
         def raw_rows(first, count):
             piece, lo = raw[first]
             return piece[:, :, lo : lo + count * CHUNK].rearrange("p j (c i) -> p c j i", i=RUN)
 
+        def operand(tier, kind, g, col, count):
+            cols = slice(col * CHUNK, (col + count) * CHUNK)
+            return codes[tier, kind, g][:, cols].bitcast(FORMAT[tier]), scales[tier, kind, g][:, cols]
+
         made = {}
 
         def quantise(tier, first, count):
-            s, lo = first // PER_SLAB, (first % PER_SLAB) * CHUNK
-            nc.vector.quantize_mx(
-                out=codes[tier, s][:, lo : lo + count * CHUNK].bitcast(FORMAT[tier]),
-                scales=scales[tier, s][:, lo : lo + count * CHUNK],
-                in_=rounded[tier, s][:, lo * PACK : (lo + count * CHUNK) * PACK],
-            )
-            for c in range(first, first + count):
-                made[tier, c] = len(made)
+            kind, g, col = chunks[first]
+            target, plane = operand(tier, kind, g, col, count)
+            nc.vector.quantize_mx(out=target, scales=plane, in_=flat(tier, first, count))
+            for i in range(count):
+                made[tier, kind, g, col + i] = len(made)
 
         back = {}
         words = {}
 
         def pass_back(target, j, first, count):
-            s, lo = first // PER_SLAB, (first % PER_SLAB) * CHUNK
+            moving, plane = operand("q", *chunks[first], count)
             nc.tensor.matmul_mx(
                 out=target,
                 lhsT=eye_codes[:, j * P : (j + 1) * P].bitcast(FORMAT["q"]),
                 lhsT_scale=eye_scales[:, j * P : (j + 1) * P],
-                rhs=codes["q", s][:, lo : lo + count * CHUNK].bitcast(FORMAT["q"]),
-                rhs_scale=scales["q", s][:, lo : lo + count * CHUNK],
+                rhs=moving,
+                rhs_scale=plane,
                 start=True,
                 stop=True,
             )
 
         def bring_back(first, count):
-            shape = [P, HALF, PAIR * CHUNK] if first in wide_pairs else [P, PACK, CHUNK]
+            wide = first in WIDE
             for c in range(first, first + count):
-                back[c] = ps.tile(shape, F32, name="back%d" % c, tag="back%d" % (c % BACK_BANKS))
+                shape = [P, HALF, PAIR * CHUNK] if wide else [P, PACK, CHUNK]
+                back[c] = ps.tile(shape, F32, name="back%d" % c, tag="back%d" % (BANK_OF.get(c, c) % BACK_BANKS))
             for j in range(PACK):
-                if first in wide_pairs:
-                    pass_back(back[first + j // HALF][:, j % HALF, :], j, first, PAIR)
+                if wide:
+                    for a in range(first, first + count, PAIR):
+                        pass_back(back[a + j // HALF][:, j % HALF, :], j, a, PAIR)
                 else:
                     for c in range(first, first + count):
                         pass_back(back[c][:, j, :], j, c, 1)
@@ -171,141 +164,259 @@ def tile_mix_tierb_four_res_kernel(tc, w, x, res, out):
             )
 
         def join_words(first):
-            lo = (first % PER_SLAB) * CHUNK * PACK
-            flat = rounded["r", first // PER_SLAB][:, lo : lo + PAIR * CHUNK * PACK]
             nc.scalar.copy(
-                out=flat.bitcast(U32).rearrange("p (c i u) -> p c u i", i=RUN, u=2),
+                out=flat("r", first, PAIR).bitcast(U32).rearrange("p (c i u) -> p c u i", i=RUN, u=2),
                 in_=words[first][:].bitcast(U32).rearrange("p (u c i) -> p c u i", i=RUN, u=2),
             )
 
+        parts = [((i,), 0, 4, "acc%d" % i) for i in range(TILES)] + [((i,), 4, 4, "acc%d" % i) for i in range(TILES - 1)]
+        parts += [((3,), 4, 2, "acc3"), ((3,), 6, 1, "back0"), ((3,), 7, 1, "back1")]
         acc = {}
-        passes_done = {}
-        closed_at = {}
+        left = {n: 8 * parts[n][2] for n in range(len(parts))}
         parked = {}
-        waiting = [
-            (h, g, i, w_tier, x_tier)
-            for h in range(T // SLAB_COLS)
-            for g in range(K // K_PASS)
-            for i in range(TILES)
-            for w_tier in "qr"
-            for x_tier in "qr"
-        ]
+        res_used = []
 
-        last_tile = [product for product in waiting if (product[0], product[2]) == (1, TILES - 1)]
-
-        def operands(product):
-            h, g, i, w_tier, x_tier = product
-            w_chunk = PER_SLAB * SLABS.index(("w", g, 0)) + i
-            x_last = PER_SLAB * SLABS.index(("x", g, h)) + PER_SLAB - 1
-            return (w_tier, w_chunk), (x_tier, x_last)
-
-        def can_run(product):
-            h, i = product[0], product[2]
-            return (h == 0 or i in parked) and all(operand in made for operand in operands(product))
-
-        def age(product):
-            return max(made[operand] for operand in operands(product))
-
-        def multiply(product, step, lo=0, cols=SLAB_COLS // 2):
-            h, g, i, w_tier, x_tier = product
-            xs, ws = SLABS.index(("x", g, h)), SLABS.index(("w", g, 0))
-            cols = cols if product in last_tile else SLAB_COLS
-            tile = (h, i, lo) if lo else (h, i)
-            done = passes_done.get(tile, 0)
-            if done == 0:
-                acc[tile] = ps.tile([P, SLAB_COLS], F32, name="acc%d_%d_%d" % (h, i, lo), tag="back%d" % (lo // CHUNK - 2) if lo else "acc%d" % i)
+        def mul(n, g, wt, xt, c=None, count=None):
+            tiles, col, width, bank = parts[n]
+            i = tiles[0]
+            c = col if c is None else c
+            count = width if count is None else count
+            first = n not in acc
+            if first:
+                acc[n] = ps.tile([P, width * CHUNK], F32, name="acc_part%d" % n, tag=bank)
+            left[n] = left[n] - count
+            assert (wt, "w", g, i) in made and all((xt, "x", g, d) in made for d in range(c, c + count)), (n, g, wt, xt)
+            stationary, stationary_plane = operand(wt, "w", g, i, 1)
+            moving, moving_plane = operand(xt, "x", g, c, count)
             nc.tensor.matmul_mx(
-                out=acc[tile][:, lo : lo + cols],
-                lhsT=codes[w_tier, ws][:, i * P : (i + 1) * P].bitcast(FORMAT[w_tier]),
-                lhsT_scale=scales[w_tier, ws][:, i * P : (i + 1) * P],
-                rhs=codes[x_tier, xs][:, lo : lo + cols].bitcast(FORMAT[x_tier]),
-                rhs_scale=scales[x_tier, xs][:, lo : lo + cols],
-                start=done == 0,
-                stop=done == PASSES_PER_TILE - 1,
+                out=acc[n][:, (c - col) * CHUNK : (c - col + count) * CHUNK],
+                lhsT=stationary,
+                lhsT_scale=stationary_plane,
+                rhs=moving,
+                rhs_scale=moving_plane,
+                start=first,
+                stop=left[n] == 0,
             )
-            passes_done[tile] = done + 1
-            if not lo:
-                if done == PASSES_PER_TILE - 1:
-                    closed_at[h, i] = step
-                waiting.remove(product)
 
-        def add_and_store(sums, h, i, parts, part=0):
-            width = SLAB_COLS // parts
-            lo = part * width
-            result = sb.tile([P, width], F32, name="result%d_%d_%d" % (h, i, part))
+        def park(n):
+            assert left[n] == 0
+            parked[n] = sb.tile([P, BANK], F32, name="parked%d" % n)
+            nc.scalar.copy(out=parked[n][:], in_=acc[n][:])
+
+        def add(n):
+            assert left[n] == 0
+            tiles, col, count, bank = parts[n]
+            i = tiles[0]
+            cols = slice(col * CHUNK, (col + count) * CHUNK)
+            result = sb.tile([P, count * CHUNK], F32, name="result%d" % n)
             nc.vector.tensor_tensor(
-                out=result[:],
-                in0=res_sb[h][:, i, lo : lo + width],
-                in1=sums[:, lo : lo + width],
-                op=mybir.AluOpType.add,
+                out=result[:], in0=res_sb[i][:, cols], in1=parked[n][:] if n in parked else acc[n][:], op=mybir.AluOpType.add
             )
-            nc.sync.dma_start(
-                out=out[i * P : (i + 1) * P, h * SLAB_COLS + lo : h * SLAB_COLS + lo + width], in_=result[:]
-            )
+            nc.sync.dma_start(out=out[i * P : (i + 1) * P, cols], in_=result[:])
 
-        stored = 0
-        for step in range(-LEAD - ROUND_LEAD, CHUNKS + 1):
-            for first, count in groups:
-                lead = LEAD + ROUND_LEAD + (PAIR if first == CHUNKS - PAIR else 0)
-                if first - lead == step and first not in vector_rounds:
-                    nc.scalar.copy(out=interleaved("q", first, count), in_=raw_rows(first, count))
-            pair, u = step - step % PAIR, step % PAIR
-            if step == last_w - LEAD:
-                quantise("q", last_w, PAIR)
-                for i in range(TILES - PAIR, TILES):
-                    multiply((0, 1, i, "q", "q"), step)
-            if pair in wide_pairs:
-                subtract_wide(pair, u)
-                if u == 1:
-                    join_words(pair)
-            elif 0 <= step < CHUNKS:
-                subtract_narrow(step)
-            ahead = [group for group in groups if group[0] - LEAD == step]
-            for group in ahead:
-                if group[0] in vector_rounds:
-                    nc.vector.tensor_copy(out=interleaved("q", *group), in_=raw_rows(*group))
-                if group[0] == 0:
-                    quantise_eye(HALF, PACK)
-                if group[0] != last_w:
-                    quantise("q", *group)
-            if step >= 1 and SLABS[(step - 1) // PER_SLAB][0] == "w":
-                quantise("r", step - 1, 1)
-            if 0 <= step < CHUNKS and SLABS[step // PER_SLAB][0] == "x" and step % PER_SLAB == PER_SLAB - 1:
-                quantise("r", pair - PAIR, PAIR)
-                if pair not in wide_pairs:
-                    quantise("r", pair, PAIR)
-            if step == CHUNKS:
-                add_and_store(parked[stored], 0, stored, 1)
-                stored = stored + 1
-            for first in wide_pairs:
-                if first % PER_SLAB == PAIR and step == min(first + 1 + JOIN_DELAY, CHUNKS):
-                    quantise("r", first, PAIR)
-            for group in ahead:
-                bring_back(*group)
-            due = [i for h, i in closed_at if h == 0 and i not in parked and closed_at[h, i] + DRAIN_DELAY <= step]
-            sums = None
-            if due:
-                sums = sb.tile([P, SLAB_COLS], F32, name="parked%d" % due[0])
-                nc.scalar.copy(out=sums[:], in_=acc[0, due[0]][:])
-            if step == CHUNKS - PER_SLAB:
-                add_and_store(parked[stored], 0, stored, 1)
-                stored = stored + 1
-            if step < CHUNKS:
-                for slot in range(PRODUCTS_PER_STEP + 1 if step < HEAD else PRODUCTS_PER_STEP):
-                    runnable = [product for product in waiting if can_run(product)]
-                    if runnable:
-                        multiply(min(runnable, key=age) if step < HEAD else runnable[0], step)
-            if due:
-                parked[due[0]] = sums
+        def rnd(c, count=1):
+            nc.scalar.copy(out=interleaved("q", c, count), in_=raw_rows(c, count))
 
-        for i in range(stored, TILES):
-            add_and_store(parked[i], 0, i, 1)
-        for i in range(TILES):
-            for product in [product for product in waiting if product[2] == i]:
-                multiply(product, CHUNKS)
-            add_and_store(acc[1, i], 1, i, 2 if i == TILES - 1 else 1)
-        for part in range(2, PER_SLAB):
-            for product in last_tile:
-                multiply(product, CHUNKS, part * CHUNK, CHUNK)
-            add_and_store(acc[1, TILES - 1, part * CHUNK], 1, TILES - 1, PER_SLAB, part)
-        assert not waiting
+        def vrnd(c, count=1):
+            nc.vector.tensor_copy(out=interleaved("q", c, count), in_=raw_rows(c, count))
+
+        def q(c, count=1):
+            quantise("q", c, count)
+
+        def r(c, count=1):
+            quantise("r", c, count)
+
+        def sub(c):
+            if c - c % 2 in WIDE:
+                subtract_wide(c - c % 2, c % 2)
+            else:
+                subtract_narrow(c)
+
+        B = bring_back
+        J = join_words
+
+        vrnd(0)
+        rnd(1)
+        q(0)
+        B(0,1)
+        q(1)
+        B(1,1)
+        rnd(3)
+        vrnd(2)
+        q(2)
+        B(2,1)
+        rnd(4)
+        rnd(5)
+        rnd(6)
+        rnd(7)
+        rnd(8,2)
+        rnd(10,2)
+        rnd(12,2)
+        rnd(14,2)
+        sub(0)
+        q(3)
+        B(3,1)
+        sub(1)
+        q(4)
+        B(4,1)
+        mul(0,0,"q","q")
+        sub(2)
+        q(5)
+        B(5,1)
+        mul(1,0,"q","q")
+        sub(3)
+        q(6)
+        B(6,1)
+        r(0,2)
+        r(2,2)
+        mul(2,0,"q","q")
+        mul(0,0,"q","r")
+        mul(1,0,"q","r")
+        mul(2,0,"q","r")
+        sub(4)
+        q(7)
+        B(7,1)
+        mul(3,0,"q","q")
+        mul(3,0,"q","r")
+        sub(5)
+        q(8,2)
+        r(4,2)
+        B(8,2)
+        mul(0,0,"r","q")
+        mul(0,0,"r","r")
+        mul(1,0,"r","q")
+        mul(1,0,"r","r")
+        sub(6)
+        sub(7)
+        q(10,2)
+        r(6,2)
+
+        sub(8)
+        B(10,2)
+        sub(9)
+        J(8)
+        q(12,2)
+        rnd(16,2)
+        mul(2,0,"r","q")
+        mul(2,0,"r","r")
+        mul(3,0,"r","q")
+        mul(3,0,"r","r")
+        sub(10)
+        B(12,2)
+        q(14,2)
+        sub(11)
+        r(8,2)
+        r(10,2)
+        rnd(18,2)
+        rnd(20,2)
+        rnd(22,2)
+        mul(0,1,"q","q")
+        mul(1,1,"q","q")
+        mul(2,1,"q","q")
+        B(14,2)
+        mul(0,1,"q","r")
+        mul(1,1,"q","r")
+        mul(2,1,"q","r")
+        sub(12)
+        sub(13)
+        q(16,2)
+        r(12,2)
+        mul(3,1,"q","q")
+        mul(3,1,"q","r")
+        B(16,2)
+        mul(0,1,"r","q")
+        mul(0,1,"r","r")
+        park(0)
+        mul(1,1,"r","q")
+        mul(1,1,"r","r")
+        park(1)
+        sub(14)
+        sub(15)
+        q(18,2)
+        r(14,2)
+        B(18,2)
+        mul(2,1,"r","q")
+        mul(2,1,"r","r")
+        sub(16)
+        sub(17)
+        J(16)
+        q(20,2)
+        mul(3,1,"r","q")
+        mul(3,1,"r","r")
+        B(20,2)
+        sub(18)
+        park(2)
+        sub(19)
+        J(18)
+        q(22,2)
+        park(3)
+        mul(4,0,"q","q")
+        mul(4,0,"r","q")
+        mul(5,0,"q","q")
+        B(22,2)
+        mul(6,0,"q","q")
+        mul(5,0,"r","q")
+        r(16,2)
+        sub(20)
+        r(18,2)
+        mul(5,0,"r","r")
+        mul(5,0,"q","r")
+        mul(4,0,"q","r")
+        mul(4,0,"r","r")
+        mul(6,0,"q","r")
+        mul(6,0,"r","q")
+        mul(6,0,"r","r")
+        mul(7,0,"q","q")
+        mul(7,0,"q","r")
+        mul(7,0,"r","q")
+        mul(7,0,"r","r")
+        sub(21)
+        J(20)
+        sub(22)
+        sub(23)
+        J(22)
+        add(0)
+        r(20,2)
+        add(1)
+        r(22,2)
+        mul(5,1,"q","q")
+        mul(4,1,"q","q")
+        mul(4,1,"r","q")
+        mul(4,1,"r","r")
+        mul(4,1,"q","r")
+        add(2)
+        add(3)
+        add(4)
+        mul(5,1,"q","r")
+        mul(5,1,"r","q")
+        mul(5,1,"r","r")
+        add(5)
+        mul(6,1,"q","q")
+        mul(6,1,"q","r")
+        mul(6,1,"r","q")
+        mul(6,1,"r","r")
+        add(6)
+        mul(7,1,"q","q")
+        mul(7,1,"q","r")
+        mul(7,1,"r","q")
+        mul(7,1,"r","r")
+        add(7)
+        mul(8,0,"q","q")
+        mul(8,0,"q","r")
+        mul(8,0,"r","q")
+        mul(8,0,"r","r")
+        mul(8,1,"q","q")
+        mul(8,1,"q","r")
+        mul(8,1,"r","q")
+        mul(8,1,"r","r")
+        add(8)
+        mul(9,0,"q","q")
+        mul(9,0,"q","r")
+        mul(9,0,"r","q")
+        mul(9,0,"r","r")
+        mul(9,1,"q","q")
+        mul(9,1,"q","r")
+        mul(9,1,"r","q")
+        mul(9,1,"r","r")
+        add(9)
+        assert not any(left.values())

@@ -23,7 +23,7 @@ RUN = 2
 HALF = PACK // 2
 HALF_RUN = 4
 
-LOADS = [(kind, g, c, 2) for g in range(2) for kind in "xw" for c in (0, 2)] + [("x", g, c, 2) for g in range(2) for c in (4, 6)] + [("res", 0, i, 0) for i in range(4)]
+LOADS = [(kind, 0, c, 2) for c in (0, 2) for kind in "xw"] + [(kind, 1, c, 2) for kind in "xw" for c in (0, 2)] + [("x", g, c, 2) for g in range(2) for c in (4, 6)] + [("res", 0, i, 0) for i in range(2)]
 HEAD = 8
 BANK_OF = {}
 WIDE = [8, 16, 18, 20, 22]
@@ -41,8 +41,10 @@ def tile_mix_tierb_four_res_kernel(tc, w, x, res, out):
         res_sb = {}
         for kind, g, first, count in LOADS:
             if kind == "res":
-                res_sb[first] = sb.tile([P, T], F32, name="res%d" % first)
-                nc.sync.dma_start(out=res_sb[first][:], in_=res[first * P : (first + 1) * P, :])
+                res_sb[first] = sb.tile([P, TILES, BANK], F32, name="res%d" % first)
+                nc.sync.dma_start(
+                    out=res_sb[first][:], in_=res[:, first * BANK : (first + 1) * BANK].rearrange("(i p) t -> p i t", p=P)
+                )
                 continue
             src = x if kind == "x" else w
             piece = sb.tile([P, PACK, count * CHUNK], F32, name="raw%d" % len(chunks), align_bytes=64)
@@ -210,7 +212,7 @@ def tile_mix_tierb_four_res_kernel(tc, w, x, res, out):
             cols = slice(col * CHUNK, (col + count) * CHUNK)
             result = sb.tile([P, count * CHUNK], F32, name="result%d" % n)
             nc.vector.tensor_tensor(
-                out=result[:], in0=res_sb[i][:, cols], in1=parked[n][:] if n in parked else acc[n][:], op=mybir.AluOpType.add
+                out=result[:], in0=res_sb[col // 4][:, i, (col % 4) * CHUNK : (col % 4 + count) * CHUNK], in1=parked[n][:] if n in parked else acc[n][:], op=mybir.AluOpType.add
             )
             nc.sync.dma_start(out=out[i * P : (i + 1) * P, cols], in_=result[:])
 
@@ -245,6 +247,7 @@ def tile_mix_tierb_four_res_kernel(tc, w, x, res, out):
         vrnd(2)
         q(2)
         B(2,1)
+        mul(0,0,"q","q",0,2)
         rnd(4)
         rnd(5)
         rnd(6)
@@ -256,155 +259,166 @@ def tile_mix_tierb_four_res_kernel(tc, w, x, res, out):
         sub(0)
         q(3)
         B(3,1)
+        mul(1,0,"q","q",0,2)
         sub(1)
         q(4)
         B(4,1)
-        mul(0,0,"q","q")
-        sub(2)
+        r(0,2)
+        mul(1,0,"q","r",0,2)
+        mul(0,0,"q","r",0,2)
         q(5)
         B(5,1)
-        mul(1,0,"q","q")
-        sub(3)
+        mul(0,0,"q","q",2,2)
+        mul(1,0,"q","q",2,2)
+        sub(2)
         q(6)
         B(6,1)
-        r(0,2)
-        r(2,2)
         mul(2,0,"q","q")
-        mul(0,0,"q","r")
-        mul(1,0,"q","r")
-        mul(2,0,"q","r")
-        sub(4)
+        mul(2,0,"q","r",0,2)
+        sub(3)
+        r(2)
         q(7)
+        r(3)
+        mul(0,0,"r","q")
+        mul(0,0,"r","r",0,2)
         B(7,1)
         mul(3,0,"q","q")
-        mul(3,0,"q","r")
+        mul(3,0,"q","r",0,2)
+        mul(1,0,"r","q")
+        mul(1,0,"r","r",0,2)
+        sub(4)
         sub(5)
         q(8,2)
         r(4,2)
         B(8,2)
-        mul(0,0,"r","q")
-        mul(0,0,"r","r")
-        mul(1,0,"r","q")
-        mul(1,0,"r","r")
+        mul(0,0,"q","r",2,2)
+        mul(0,0,"r","r",2,2)
+        mul(1,0,"q","r",2,2)
+        mul(1,0,"r","r",2,2)
+        mul(2,0,"q","r",2,2)
+        mul(3,0,"q","r",2,2)
         sub(6)
-        sub(7)
         q(10,2)
-        r(6,2)
-
-        sub(8)
-        B(10,2)
-        sub(9)
-        J(8)
-        q(12,2)
-        rnd(16,2)
+        B(10,1)
+        sub(7)
+        r(6)
+        B(11,1)
         mul(2,0,"r","q")
         mul(2,0,"r","r")
+
+        sub(8)
+        r(7)
+        q(12,2)
         mul(3,0,"r","q")
         mul(3,0,"r","r")
-        sub(10)
-        B(12,2)
+        mul(0,1,"q","q")
+        mul(1,1,"q","q")
+        sub(9)
+        J(8)
         q(14,2)
+        rnd(16,2)
+        B(12,2)
+        mul(2,1,"q","q")
+        mul(3,1,"q","q")
+        sub(10)
         sub(11)
         r(8,2)
         r(10,2)
         rnd(18,2)
         rnd(20,2)
         rnd(22,2)
-        mul(0,1,"q","q")
-        mul(1,1,"q","q")
-        mul(2,1,"q","q")
         B(14,2)
+        mul(3,1,"q","r")
         mul(0,1,"q","r")
         mul(1,1,"q","r")
         mul(2,1,"q","r")
         sub(12)
-        sub(13)
         q(16,2)
-        r(12,2)
-        mul(3,1,"q","q")
-        mul(3,1,"q","r")
+        sub(13)
+        r(12)
         B(16,2)
         mul(0,1,"r","q")
         mul(0,1,"r","r")
         park(0)
+        sub(14)
+        r(13)
+        q(18,2)
         mul(1,1,"r","q")
         mul(1,1,"r","r")
         park(1)
-        sub(14)
         sub(15)
-        q(18,2)
-        r(14,2)
+        r(14)
         B(18,2)
         mul(2,1,"r","q")
         mul(2,1,"r","r")
         sub(16)
-        sub(17)
-        J(16)
+        r(15)
         q(20,2)
         mul(3,1,"r","q")
         mul(3,1,"r","r")
+        sub(17)
+        J(16)
         B(20,2)
+
         sub(18)
-        park(2)
         sub(19)
         J(18)
         q(22,2)
-        park(3)
+        add(2)
         mul(4,0,"q","q")
         mul(4,0,"r","q")
         mul(5,0,"q","q")
-        B(22,2)
-        mul(6,0,"q","q")
         mul(5,0,"r","q")
+        B(22,2)
+        mul(4,1,"q","q")
+        mul(4,1,"r","q")
         r(16,2)
         sub(20)
         r(18,2)
-        mul(5,0,"r","r")
-        mul(5,0,"q","r")
-        mul(4,0,"q","r")
-        mul(4,0,"r","r")
+        mul(5,1,"q","q")
+        mul(5,1,"r","q")
+        mul(6,0,"q","q")
         mul(6,0,"q","r")
         mul(6,0,"r","q")
         mul(6,0,"r","r")
-        mul(7,0,"q","q")
-        mul(7,0,"q","r")
-        mul(7,0,"r","q")
-        mul(7,0,"r","r")
+        mul(4,0,"q","r")
+        mul(4,0,"r","r")
+        mul(5,0,"q","r")
+        mul(5,0,"r","r")
         sub(21)
         J(20)
         sub(22)
         sub(23)
         J(22)
-        add(0)
-        r(20,2)
-        add(1)
-        r(22,2)
-        mul(5,1,"q","q")
-        mul(4,1,"q","q")
-        mul(4,1,"r","q")
-        mul(4,1,"r","r")
-        mul(4,1,"q","r")
-        add(2)
         add(3)
+        mul(6,1,"q","q")
+        mul(6,1,"r","q")
+        mul(8,0,"q","q")
+        mul(8,0,"q","r")
+        mul(8,0,"r","q")
+        mul(8,0,"r","r")
+        r(20,2)
+        add(0)
+        r(22,2)
+        mul(4,1,"q","r")
+        mul(4,1,"r","r")
+        add(1)
         add(4)
         mul(5,1,"q","r")
-        mul(5,1,"r","q")
         mul(5,1,"r","r")
         add(5)
-        mul(6,1,"q","q")
         mul(6,1,"q","r")
-        mul(6,1,"r","q")
         mul(6,1,"r","r")
         add(6)
+        mul(7,0,"q","q")
+        mul(7,0,"q","r")
+        mul(7,0,"r","q")
+        mul(7,0,"r","r")
         mul(7,1,"q","q")
         mul(7,1,"q","r")
         mul(7,1,"r","q")
         mul(7,1,"r","r")
         add(7)
-        mul(8,0,"q","q")
-        mul(8,0,"q","r")
-        mul(8,0,"r","q")
-        mul(8,0,"r","r")
         mul(8,1,"q","q")
         mul(8,1,"q","r")
         mul(8,1,"r","q")

@@ -7,9 +7,11 @@ FLOPS = 4 * 2 * K * N * T
 
 F32 = mybir.dt.float32
 BF16 = mybir.dt.bfloat16
+I32 = mybir.dt.int32
 U32 = mybir.dt.uint32
 U8 = mybir.dt.uint8
 FORMAT = {"q": mybir.dt.float8_e4m3fn_x4, "r": mybir.dt.float8_e5m2_x4}
+BF16_ONE = 0x3F80
 
 P = 128
 PACK = 4
@@ -17,16 +19,25 @@ K_PASS = P * PACK
 BANK = 512
 CHUNK = 128
 PAIR = 2
+SLAB = BANK // CHUNK
 TILES = N // P
-BACK_BANKS = 4
+BACK_BANKS = 8 - TILES
+PRODUCTS = 4 * (K // K_PASS)
 RUN = 2
 HALF = PACK // 2
 HALF_RUN = 4
 
-LOADS = [(kind, 0, c, 2) for c in (0, 2) for kind in "xw"] + [(kind, 1, c, 2) for kind in "xw" for c in (0, 2)] + [("x", g, c, 2) for g in range(2) for c in (4, 6)] + [("res", 0, i, 0) for i in range(2)]
-HEAD = 8
-BANK_OF = {}
-WIDE = [8, 16, 18, 20, 22]
+LOADS = [(kind, 0, col) for col in (0, PAIR) for kind in "xw"]
+LOADS = LOADS + [(kind, 1, col) for kind in "xw" for col in (0, PAIR)]
+LOADS = LOADS + [("x", g, col) for g in range(K // K_PASS) for col in (SLAB, SLAB + PAIR)]
+X_A, W_A, X_B, W_B = range(0, 2 * SLAB, PAIR)
+X_K1, W_K1, X_T0, X_T1 = range(2 * SLAB, 6 * SLAB, SLAB)
+WIDE = [X_K1, X_T0, X_T0 + PAIR, X_T1, X_T1 + PAIR]
+LAST = TILES - 1
+PARTS = [(i, 0, SLAB, "acc%d" % i) for i in range(TILES)] + [(i, SLAB, SLAB, "acc%d" % i) for i in range(LAST)]
+PARTS = PARTS + [(LAST, SLAB, PAIR, "acc%d" % LAST), (LAST, SLAB + 2, 1, "back0"), (LAST, SLAB + 3, 1, "back1")]
+SECOND = TILES
+LAST_HALF, QUARTER_A, QUARTER_B = range(SECOND + LAST, len(PARTS))
 
 
 def tile_mix_tierb_four_res_kernel(tc, w, x, res, out):
@@ -38,27 +49,18 @@ def tile_mix_tierb_four_res_kernel(tc, w, x, res, out):
 
         chunks = []
         raw = []
-        res_sb = {}
-        for kind, g, first, count in LOADS:
-            if kind == "res":
-                res_sb[first] = sb.tile([P, TILES, BANK], F32, name="res%d" % first)
-                nc.sync.dma_start(
-                    out=res_sb[first][:], in_=res[:, first * BANK : (first + 1) * BANK].rearrange("(i p) t -> p i t", p=P)
-                )
-                continue
+        for kind, g, col in LOADS:
             src = x if kind == "x" else w
-            piece = sb.tile([P, PACK, count * CHUNK], F32, name="raw%d" % len(chunks), align_bytes=64)
-            nc.sync.dma_start(
-                out=piece[:],
-                in_=src[g * K_PASS : (g + 1) * K_PASS, first * CHUNK : (first + count) * CHUNK].rearrange(
-                    "(p j) c -> p j c", j=PACK
-                ),
-            )
-            for i in range(count):
-                chunks.append((kind, g, first + i))
+            piece = sb.tile([P, PACK, PAIR * CHUNK], F32, name="raw%d" % len(chunks), align_bytes=64)
+            rows = src[g * K_PASS : (g + 1) * K_PASS, col * CHUNK : (col + PAIR) * CHUNK]
+            nc.sync.dma_start(out=piece[:], in_=rows.rearrange("(p j) c -> p j c", j=PACK))
+            for i in range(PAIR):
+                chunks.append((kind, g, col + i))
                 raw.append((piece, i * CHUNK))
-        last = len(chunks)
-        groups = [(c, 1) for c in range(HEAD)] + [(c, PAIR) for c in range(HEAD, last, PAIR)]
+        res_sb = {}
+        for h in range(T // BANK):
+            res_sb[h] = sb.tile([P, TILES, BANK], F32, name="res%d" % h)
+            nc.sync.dma_start(out=res_sb[h][:], in_=res[:, h * BANK : (h + 1) * BANK].rearrange("(i p) t -> p i t", p=P))
 
         eye = sb.tile([P, PACK * K_PASS], BF16, name="eye", align_bytes=64)
         eye_codes = sb.tile([P, K_PASS], U32, name="eye_codes", align_bytes=256)
@@ -69,10 +71,10 @@ def tile_mix_tierb_four_res_kernel(tc, w, x, res, out):
         )
         for j in range(PACK):
             nc.vector.tensor_scalar(
-                out=eye[:, j * K_PASS : (j + 1) * K_PASS].bitcast(mybir.dt.int32),
+                out=eye[:, j * K_PASS : (j + 1) * K_PASS].bitcast(I32),
                 in0=ramp[:],
                 scalar1=float(j // HALF),
-                scalar2=float(0x3F80 << (16 * (j % HALF))),
+                scalar2=float(BF16_ONE << (16 * (j % HALF))),
                 op0=mybir.AluOpType.is_equal,
                 op1=mybir.AluOpType.mult,
             )
@@ -109,14 +111,19 @@ def tile_mix_tierb_four_res_kernel(tc, w, x, res, out):
             cols = slice(col * CHUNK, (col + count) * CHUNK)
             return codes[tier, kind, g][:, cols].bitcast(FORMAT[tier]), scales[tier, kind, g][:, cols]
 
-        made = {}
+        def round_on_scalar(first, count=1):
+            nc.scalar.copy(out=interleaved("q", first, count), in_=raw_rows(first, count))
 
-        def quantise(tier, first, count):
+        def round_on_vector(first):
+            nc.vector.tensor_copy(out=interleaved("q", first, 1), in_=raw_rows(first, 1))
+
+        made = []
+
+        def quantise(tier, first, count=1):
             kind, g, col = chunks[first]
             target, plane = operand(tier, kind, g, col, count)
             nc.vector.quantize_mx(out=target, scales=plane, in_=flat(tier, first, count))
-            for i in range(count):
-                made[tier, kind, g, col + i] = len(made)
+            made.extend((tier, kind, g, col + i) for i in range(count))
 
         back = {}
         words = {}
@@ -133,37 +140,30 @@ def tile_mix_tierb_four_res_kernel(tc, w, x, res, out):
                 stop=True,
             )
 
-        def bring_back(first, count):
-            wide = first in WIDE
+        def bring_back(first, count=1):
+            shape = [P, HALF, PAIR * CHUNK] if first in WIDE else [P, PACK, CHUNK]
             for c in range(first, first + count):
-                shape = [P, HALF, PAIR * CHUNK] if wide else [P, PACK, CHUNK]
-                back[c] = ps.tile(shape, F32, name="back%d" % c, tag="back%d" % (BANK_OF.get(c, c) % BACK_BANKS))
+                back[c] = ps.tile(shape, F32, name="back%d" % c, tag="back%d" % (c % BACK_BANKS))
             for j in range(PACK):
-                if wide:
-                    for a in range(first, first + count, PAIR):
-                        pass_back(back[a + j // HALF][:, j % HALF, :], j, a, PAIR)
+                if first in WIDE:
+                    pass_back(back[first + j // HALF][:, j % HALF, :], j, first, PAIR)
                 else:
                     for c in range(first, first + count):
                         pass_back(back[c][:, j, :], j, c, 1)
 
-        def subtract_narrow(c):
-            nc.vector.tensor_tensor(
-                out=interleaved("r", c, 1),
-                in0=raw_rows(c, 1),
-                in1=back[c][:].rearrange("p j (c i) -> p c j i", i=RUN),
-                op=mybir.AluOpType.subtract,
-            )
-
-        def subtract_wide(first, u):
-            width = HALF * PAIR * CHUNK
-            if u == 0:
-                words[first] = sb.tile([P, 2 * width], BF16, name="words%d" % first, align_bytes=64)
-            nc.vector.tensor_tensor(
-                out=words[first][:, u * width : (u + 1) * width].rearrange("p (c i e) -> p c e i", i=HALF_RUN, e=HALF),
-                in0=raw[first][0][:, HALF * u : HALF * (u + 1), :].rearrange("p e (c i) -> p c e i", i=HALF_RUN),
-                in1=back[first + u][:].rearrange("p e (c i) -> p c e i", i=HALF_RUN),
-                op=mybir.AluOpType.subtract,
-            )
+        def subtract(c):
+            first, u = c - c % PAIR, c % PAIR
+            if first not in WIDE:
+                target, source = interleaved("r", c, 1), raw_rows(c, 1)
+                values = back[c][:].rearrange("p j (c i) -> p c j i", i=RUN)
+            else:
+                width = HALF * PAIR * CHUNK
+                if u == 0:
+                    words[first] = sb.tile([P, 2 * width], BF16, name="words%d" % first, align_bytes=64)
+                target = words[first][:, u * width : (u + 1) * width].rearrange("p (c i e) -> p c e i", i=HALF_RUN, e=HALF)
+                source = raw[first][0][:, HALF * u : HALF * (u + 1), :].rearrange("p e (c i) -> p c e i", i=HALF_RUN)
+                values = back[c][:].rearrange("p e (c i) -> p c e i", i=HALF_RUN)
+            nc.vector.tensor_tensor(out=target, in0=source, in1=values, op=mybir.AluOpType.subtract)
 
         def join_words(first):
             nc.scalar.copy(
@@ -171,266 +171,183 @@ def tile_mix_tierb_four_res_kernel(tc, w, x, res, out):
                 in_=words[first][:].bitcast(U32).rearrange("p (u c i) -> p c u i", i=RUN, u=2),
             )
 
-        parts = [((i,), 0, 4, "acc%d" % i) for i in range(TILES)] + [((i,), 4, 4, "acc%d" % i) for i in range(TILES - 1)]
-        parts += [((3,), 4, 2, "acc3"), ((3,), 6, 1, "back0"), ((3,), 7, 1, "back1")]
         acc = {}
-        left = {n: 8 * parts[n][2] for n in range(len(parts))}
+        left = [PRODUCTS * count for i, col, count, bank in PARTS]
         parked = {}
-        res_used = []
 
-        def mul(n, g, wt, xt, c=None, count=None):
-            tiles, col, width, bank = parts[n]
-            i = tiles[0]
-            c = col if c is None else c
-            count = width if count is None else count
-            first = n not in acc
-            if first:
-                acc[n] = ps.tile([P, width * CHUNK], F32, name="acc_part%d" % n, tag=bank)
-            left[n] = left[n] - count
-            assert (wt, "w", g, i) in made and all((xt, "x", g, d) in made for d in range(c, c + count)), (n, g, wt, xt)
-            stationary, stationary_plane = operand(wt, "w", g, i, 1)
-            moving, moving_plane = operand(xt, "x", g, c, count)
-            nc.tensor.matmul_mx(
-                out=acc[n][:, (c - col) * CHUNK : (c - col + count) * CHUNK],
-                lhsT=stationary,
-                lhsT_scale=stationary_plane,
-                rhs=moving,
-                rhs_scale=moving_plane,
-                start=first,
-                stop=left[n] == 0,
-            )
+        def multiply(part, g, tiers, pair=None):
+            i, col, count, bank = PARTS[part]
+            lo, count = (0, count) if pair is None else (pair * PAIR, PAIR)
+            for w_tier, x_tier in tiers.split():
+                opens = part not in acc
+                if opens:
+                    acc[part] = ps.tile([P, PARTS[part][2] * CHUNK], F32, name="acc_part%d" % part, tag=bank)
+                left[part] = left[part] - count
+                assert (w_tier, "w", g, i) in made and (x_tier, "x", g, col + lo + count - 1) in made
+                stationary, stationary_plane = operand(w_tier, "w", g, i, 1)
+                moving, moving_plane = operand(x_tier, "x", g, col + lo, count)
+                nc.tensor.matmul_mx(
+                    out=acc[part][:, lo * CHUNK : (lo + count) * CHUNK],
+                    lhsT=stationary,
+                    lhsT_scale=stationary_plane,
+                    rhs=moving,
+                    rhs_scale=moving_plane,
+                    start=opens,
+                    stop=left[part] == 0,
+                )
 
-        def park(n):
-            assert left[n] == 0
-            parked[n] = sb.tile([P, BANK], F32, name="parked%d" % n)
-            nc.scalar.copy(out=parked[n][:], in_=acc[n][:])
+        def park(part):
+            assert left[part] == 0
+            parked[part] = sb.tile([P, BANK], F32, name="parked%d" % part)
+            nc.scalar.copy(out=parked[part][:], in_=acc[part][:])
 
-        def add(n):
-            assert left[n] == 0
-            tiles, col, count, bank = parts[n]
-            i = tiles[0]
-            cols = slice(col * CHUNK, (col + count) * CHUNK)
-            result = sb.tile([P, count * CHUNK], F32, name="result%d" % n)
+        def add_and_store(part):
+            assert left[part] == 0
+            i, col, count, bank = PARTS[part]
+            lo, width = (col % SLAB) * CHUNK, count * CHUNK
+            result = sb.tile([P, width], F32, name="result%d" % part)
             nc.vector.tensor_tensor(
-                out=result[:], in0=res_sb[col // 4][:, i, (col % 4) * CHUNK : (col % 4 + count) * CHUNK], in1=parked[n][:] if n in parked else acc[n][:], op=mybir.AluOpType.add
+                out=result[:],
+                in0=res_sb[col // SLAB][:, i, lo : lo + width],
+                in1=parked[part][:] if part in parked else acc[part][:],
+                op=mybir.AluOpType.add,
             )
-            nc.sync.dma_start(out=out[i * P : (i + 1) * P, cols], in_=result[:])
+            nc.sync.dma_start(out=out[i * P : (i + 1) * P, col * CHUNK : col * CHUNK + width], in_=result[:])
 
-        def rnd(c, count=1):
-            nc.scalar.copy(out=interleaved("q", c, count), in_=raw_rows(c, count))
+        round_on_vector(X_A)
+        round_on_scalar(X_A + 1)
+        for c in (X_A, X_A + 1):
+            quantise("q", c)
+            bring_back(c)
+        round_on_scalar(W_A + 1)
+        round_on_vector(W_A)
+        quantise("q", W_A)
+        bring_back(W_A)
+        multiply(0, 0, "qq", pair=0)
+        for c in range(X_B, X_K1):
+            round_on_scalar(c)
+        for first in range(X_K1, X_T0, PAIR):
+            round_on_scalar(first, PAIR)
+        subtract(X_A)
+        quantise("q", W_A + 1)
+        bring_back(W_A + 1)
+        multiply(1, 0, "qq", pair=0)
+        subtract(X_A + 1)
+        quantise("r", X_A)
+        quantise("q", X_B)
+        bring_back(X_B)
+        quantise("r", X_A + 1)
+        for i in (1, 0):
+            multiply(i, 0, "qr", pair=0)
+        quantise("q", X_B + 1)
+        bring_back(X_B + 1)
+        for i in (0, 1):
+            multiply(i, 0, "qq", pair=1)
+        subtract(W_A)
+        quantise("q", W_B)
+        bring_back(W_B)
+        multiply(2, 0, "qq")
+        multiply(2, 0, "qr", pair=0)
+        subtract(W_A + 1)
+        quantise("r", W_A)
+        quantise("q", W_B + 1)
+        quantise("r", W_A + 1)
+        multiply(0, 0, "rq")
+        multiply(0, 0, "rr", pair=0)
+        bring_back(W_B + 1)
+        multiply(3, 0, "qq")
+        multiply(3, 0, "qr", pair=0)
+        multiply(1, 0, "rq")
+        multiply(1, 0, "rr", pair=0)
+        subtract(X_B)
+        subtract(X_B + 1)
+        quantise("q", X_K1, PAIR)
+        quantise("r", X_B, PAIR)
+        bring_back(X_K1, PAIR)
+        for i in range(TILES):
+            multiply(i, 0, "qr rr" if i < PAIR else "qr", pair=1)
+        subtract(W_B)
+        quantise("q", X_K1 + PAIR, PAIR)
+        bring_back(X_K1 + PAIR)
+        subtract(W_B + 1)
+        quantise("r", W_B)
+        bring_back(X_K1 + PAIR + 1)
+        multiply(2, 0, "rq rr")
 
-        def vrnd(c, count=1):
-            nc.vector.tensor_copy(out=interleaved("q", c, count), in_=raw_rows(c, count))
-
-        def q(c, count=1):
-            quantise("q", c, count)
-
-        def r(c, count=1):
-            quantise("r", c, count)
-
-        def sub(c):
-            if c - c % 2 in WIDE:
-                subtract_wide(c - c % 2, c % 2)
+        subtract(X_K1)
+        quantise("r", W_B + 1)
+        quantise("q", W_K1, PAIR)
+        multiply(3, 0, "rq rr")
+        for i in (0, 1):
+            multiply(i, 1, "qq")
+        subtract(X_K1 + 1)
+        join_words(X_K1)
+        quantise("q", W_K1 + PAIR, PAIR)
+        round_on_scalar(X_T0, PAIR)
+        bring_back(W_K1, PAIR)
+        for i in (2, 3):
+            multiply(i, 1, "qq")
+        subtract(X_K1 + 2)
+        subtract(X_K1 + 3)
+        for first in (X_K1, X_K1 + PAIR):
+            quantise("r", first, PAIR)
+        for first in range(X_T0 + PAIR, len(chunks), PAIR):
+            round_on_scalar(first, PAIR)
+        bring_back(W_K1 + PAIR, PAIR)
+        for i in (3, 0, 1, 2):
+            multiply(i, 1, "qr")
+        subtract(W_K1)
+        quantise("q", X_T0, PAIR)
+        for i in range(TILES):
+            subtract(W_K1 + i + 1)
+            quantise("r", W_K1 + i)
+            if i % PAIR == 0:
+                bring_back(X_T0 + i, PAIR)
             else:
-                subtract_narrow(c)
+                quantise("q", X_T0 + i + 1, PAIR)
+            multiply(i, 1, "rq rr")
+            if i < PAIR:
+                park(i)
 
-        B = bring_back
-        J = join_words
+        subtract(X_T0 + 1)
+        join_words(X_T0)
+        bring_back(X_T1, PAIR)
+        subtract(X_T0 + 2)
+        park(2)
+        subtract(X_T0 + 3)
+        join_words(X_T0 + PAIR)
+        quantise("q", X_T1 + PAIR, PAIR)
+        for i in (0, 1):
+            multiply(SECOND + i, 0, "qq rq")
+        bring_back(X_T1 + PAIR, PAIR)
+        multiply(SECOND, 1, "qq rq")
+        quantise("r", X_T0, PAIR)
+        subtract(X_T1)
+        subtract(X_T1 + 1)
+        join_words(X_T1)
+        quantise("r", X_T0 + PAIR, PAIR)
+        multiply(SECOND + 1, 1, "qq rq")
+        multiply(SECOND + 2, 0, "qq qr rq rr")
+        for i in (0, 1):
+            multiply(SECOND + i, 0, "qr rr")
+        subtract(X_T1 + 2)
+        subtract(X_T1 + 3)
+        join_words(X_T1 + PAIR)
+        add_and_store(0)
+        multiply(SECOND + 2, 1, "qq rq")
+        multiply(QUARTER_A, 0, "qq qr rq rr")
+        quantise("r", X_T1, PAIR)
+        add_and_store(1)
+        quantise("r", X_T1 + PAIR, PAIR)
 
-        vrnd(0)
-        rnd(1)
-        q(0)
-        B(0,1)
-        q(1)
-        B(1,1)
-        rnd(3)
-        vrnd(2)
-        q(2)
-        B(2,1)
-        mul(0,0,"q","q",0,2)
-        rnd(4)
-        rnd(5)
-        rnd(6)
-        rnd(7)
-        rnd(8,2)
-        rnd(10,2)
-        rnd(12,2)
-        rnd(14,2)
-        sub(0)
-        q(3)
-        B(3,1)
-        mul(1,0,"q","q",0,2)
-        sub(1)
-        q(4)
-        B(4,1)
-        r(0,2)
-        mul(1,0,"q","r",0,2)
-        mul(0,0,"q","r",0,2)
-        q(5)
-        B(5,1)
-        mul(0,0,"q","q",2,2)
-        mul(1,0,"q","q",2,2)
-        sub(2)
-        q(6)
-        B(6,1)
-        mul(2,0,"q","q")
-        mul(2,0,"q","r",0,2)
-        sub(3)
-        r(2)
-        q(7)
-        r(3)
-        mul(0,0,"r","q")
-        mul(0,0,"r","r",0,2)
-        B(7,1)
-        mul(3,0,"q","q")
-        mul(3,0,"q","r",0,2)
-        mul(1,0,"r","q")
-        mul(1,0,"r","r",0,2)
-        sub(4)
-        sub(5)
-        q(8,2)
-        r(4,2)
-        B(8,2)
-        mul(0,0,"q","r",2,2)
-        mul(0,0,"r","r",2,2)
-        mul(1,0,"q","r",2,2)
-        mul(1,0,"r","r",2,2)
-        mul(2,0,"q","r",2,2)
-        mul(3,0,"q","r",2,2)
-        sub(6)
-        q(10,2)
-        B(10,1)
-        sub(7)
-        r(6)
-        B(11,1)
-        mul(2,0,"r","q")
-        mul(2,0,"r","r")
-
-        sub(8)
-        r(7)
-        q(12,2)
-        mul(3,0,"r","q")
-        mul(3,0,"r","r")
-        mul(0,1,"q","q")
-        mul(1,1,"q","q")
-        sub(9)
-        J(8)
-        q(14,2)
-        rnd(16,2)
-        B(12,2)
-        mul(2,1,"q","q")
-        mul(3,1,"q","q")
-        sub(10)
-        sub(11)
-        r(8,2)
-        r(10,2)
-        rnd(18,2)
-        rnd(20,2)
-        rnd(22,2)
-        B(14,2)
-        mul(3,1,"q","r")
-        mul(0,1,"q","r")
-        mul(1,1,"q","r")
-        mul(2,1,"q","r")
-        sub(12)
-        q(16,2)
-        sub(13)
-        r(12)
-        B(16,2)
-        mul(0,1,"r","q")
-        mul(0,1,"r","r")
-        park(0)
-        sub(14)
-        r(13)
-        q(18,2)
-        mul(1,1,"r","q")
-        mul(1,1,"r","r")
-        park(1)
-        sub(15)
-        r(14)
-        B(18,2)
-        mul(2,1,"r","q")
-        mul(2,1,"r","r")
-        sub(16)
-        r(15)
-        q(20,2)
-        mul(3,1,"r","q")
-        mul(3,1,"r","r")
-        sub(17)
-        J(16)
-        B(20,2)
-
-        sub(18)
-        sub(19)
-        J(18)
-        q(22,2)
-        add(2)
-        mul(4,0,"q","q")
-        mul(4,0,"r","q")
-        mul(5,0,"q","q")
-        mul(5,0,"r","q")
-        B(22,2)
-        mul(4,1,"q","q")
-        mul(4,1,"r","q")
-        r(16,2)
-        sub(20)
-        r(18,2)
-        mul(5,1,"q","q")
-        mul(5,1,"r","q")
-        mul(6,0,"q","q")
-        mul(6,0,"q","r")
-        mul(6,0,"r","q")
-        mul(6,0,"r","r")
-        mul(4,0,"q","r")
-        mul(4,0,"r","r")
-        mul(5,0,"q","r")
-        mul(5,0,"r","r")
-        sub(21)
-        J(20)
-        sub(22)
-        sub(23)
-        J(22)
-        add(3)
-        mul(6,1,"q","q")
-        mul(6,1,"r","q")
-        mul(8,0,"q","q")
-        mul(8,0,"q","r")
-        mul(8,0,"r","q")
-        mul(8,0,"r","r")
-        r(20,2)
-        add(0)
-        r(22,2)
-        mul(4,1,"q","r")
-        mul(4,1,"r","r")
-        add(1)
-        add(4)
-        mul(5,1,"q","r")
-        mul(5,1,"r","r")
-        add(5)
-        mul(6,1,"q","r")
-        mul(6,1,"r","r")
-        add(6)
-        mul(7,0,"q","q")
-        mul(7,0,"q","r")
-        mul(7,0,"r","q")
-        mul(7,0,"r","r")
-        mul(7,1,"q","q")
-        mul(7,1,"q","r")
-        mul(7,1,"r","q")
-        mul(7,1,"r","r")
-        add(7)
-        mul(8,1,"q","q")
-        mul(8,1,"q","r")
-        mul(8,1,"r","q")
-        mul(8,1,"r","r")
-        add(8)
-        mul(9,0,"q","q")
-        mul(9,0,"q","r")
-        mul(9,0,"r","q")
-        mul(9,0,"r","r")
-        mul(9,1,"q","q")
-        mul(9,1,"q","r")
-        mul(9,1,"r","q")
-        mul(9,1,"r","r")
-        add(9)
-        assert not any(left.values())
+        multiply(SECOND, 1, "qr rr")
+        for part in (2, 3, SECOND):
+            add_and_store(part)
+        for part in (SECOND + 1, SECOND + 2):
+            multiply(part, 1, "qr rr")
+            add_and_store(part)
+        for part in (LAST_HALF, QUARTER_A, QUARTER_B):
+            for g in range(1 if part == QUARTER_A else 0, K // K_PASS):
+                multiply(part, g, "qq qr rq rr")
+            add_and_store(part)
+        assert not any(left)

@@ -26,6 +26,7 @@ PRODUCTS = 4 * (K // K_PASS)
 RUN = 2
 HALF = PACK // 2
 HALF_RUN = 4
+LINE_RUN = 4
 
 LOADS = [(kind, 0, col) for col in (0, PAIR) for kind in "xw"]
 LOADS = LOADS + [(kind, 1, col) for kind in "xw" for col in (0, PAIR)]
@@ -100,19 +101,19 @@ def tile_mix_tierb_four_res_kernel(tc, w, x, res, out):
             kind, g, col = chunks[first]
             return rounded[tier, kind, g][:, col * CHUNK * PACK : (col + count) * CHUNK * PACK]
 
-        def interleaved(tier, first, count):
-            return flat(tier, first, count).rearrange("p (c i j) -> p c j i", i=RUN, j=PACK)
+        def interleaved(tier, first, count, run=RUN):
+            return flat(tier, first, count).rearrange("p (c i j) -> p c j i", i=run, j=PACK)
 
-        def raw_rows(first, count):
+        def raw_rows(first, count, run=RUN):
             piece, lo = raw[first]
-            return piece[:, :, lo : lo + count * CHUNK].rearrange("p j (c i) -> p c j i", i=RUN)
+            return piece[:, :, lo : lo + count * CHUNK].rearrange("p j (c i) -> p c j i", i=run)
 
         def operand(tier, kind, g, col, count):
             cols = slice(col * CHUNK, (col + count) * CHUNK)
             return codes[tier, kind, g][:, cols].bitcast(FORMAT[tier]), scales[tier, kind, g][:, cols]
 
         def round_on_scalar(first, count=1):
-            nc.scalar.copy(out=interleaved("q", first, count), in_=raw_rows(first, count))
+            nc.scalar.copy(out=interleaved("q", first, count, LINE_RUN), in_=raw_rows(first, count, LINE_RUN))
 
         def round_on_vector(first):
             nc.vector.tensor_copy(out=interleaved("q", first, 1), in_=raw_rows(first, 1))

@@ -166,6 +166,15 @@ def tile_mix_tierb_four_res_kernel(tc, w, x, res, out):
                 values = back[c][:].rearrange("p e (c i) -> p c e i", i=HALF_RUN)
             nc.vector.tensor_tensor(out=target, in0=source, in1=values, op=mybir.AluOpType.subtract)
 
+        def subtract_half(c, half):
+            runs = slice(half * CHUNK // (2 * RUN), (half + 1) * CHUNK // (2 * RUN))
+            nc.vector.tensor_tensor(
+                out=interleaved("r", c, 1)[:, runs],
+                in0=raw_rows(c, 1)[:, runs],
+                in1=back[c][:].rearrange("p j (c i) -> p c j i", i=RUN)[:, runs],
+                op=mybir.AluOpType.subtract,
+            )
+
         def join_words(first):
             nc.scalar.copy(
                 out=flat("r", first, PAIR).bitcast(U32).rearrange("p (c i u) -> p c u i", i=RUN, u=2),
@@ -240,16 +249,18 @@ def tile_mix_tierb_four_res_kernel(tc, w, x, res, out):
         quantise("r", X_A + 1)
         for i in (1, 0):
             multiply(i, 0, "qr", pair=0)
+        subtract_half(W_A, 0)
         quantise("q", X_B + 1)
         bring_back(X_B + 1)
         for i in (0, 1):
             multiply(i, 0, "qq", pair=1)
-        subtract(W_A)
+        subtract_half(W_A, 1)
+        subtract_half(W_A + 1, 0)
         quantise("q", W_B)
         bring_back(W_B)
         multiply(2, 0, "qq")
         multiply(2, 0, "qr", pair=0)
-        subtract(W_A + 1)
+        subtract_half(W_A + 1, 1)
         quantise("r", W_A)
         quantise("q", W_B + 1)
         quantise("r", W_A + 1)

from contextlib import ExitStack

import concourse.mybir as mybir

K, N, T = 1024, 512, 1024
FLOPS = 4 * 2 * K * N * T

F32 = mybir.dt.float32
BF16 = mybir.dt.bfloat16
I32 = mybir.dt.int32
U32 = mybir.dt.uint32
U8 = mybir.dt.uint8
FORMAT = {"q": mybir.dt.float8_e4m3fn_x4, "r": mybir.dt.float8_e5m2_x4}
BF16_ONE = 0x3F80

P = 128
PACK = 4
K_PASS = P * PACK
BANK = 512
CHUNK = 128
PAIR = 2
SLAB = BANK // CHUNK
TILES = N // P
BACK_BANKS = 8 - TILES
PRODUCTS = 4 * (K // K_PASS)
RUN = 2
HALF = PACK // 2
HALF_RUN = 4
LINE_RUN = 4

LOADS = [(kind, 0, col) for col in (0, PAIR) for kind in "xw"]
LOADS = LOADS + [(kind, 1, col) for kind in "xw" for col in (0, PAIR)]
LOADS = LOADS + [("x", g, col) for g in range(K // K_PASS) for col in (SLAB, SLAB + PAIR)]
X_A, W_A, X_B, W_B = range(0, 2 * SLAB, PAIR)
X_K1, W_K1, X_T0, X_T1 = range(2 * SLAB, 6 * SLAB, SLAB)
WIDE = [X_K1, X_T0, X_T0 + PAIR, X_T1, X_T1 + PAIR]
LAST = TILES - 1
PARTS = [(i, 0, SLAB, "acc%d" % i) for i in range(TILES)] + [(i, SLAB, SLAB, "acc%d" % i) for i in range(LAST)]
PARTS = PARTS + [(LAST, SLAB, PAIR, "acc%d" % LAST), (LAST, SLAB + 2, 1, "back0"), (LAST, SLAB + 3, 1, "back1")]
SECOND = TILES
LAST_HALF, QUARTER_A, QUARTER_B = range(SECOND + LAST, len(PARTS))


def tile_mix_tierb_four_res_kernel(tc, w, x, res, out):
    nc = tc.nc
    with ExitStack() as ctx:
        sb = ctx.enter_context(tc.tile_pool(name="sb", bufs=1))
        ps = ctx.enter_context(tc.psum_pool(name="ps", bufs=1))
        ctx.enter_context(tc.manual_schedule())

        chunks = []
        raw = []
        for kind, g, col in LOADS:
            src = x if kind == "x" else w
            piece = sb.tile([P, PACK, PAIR * CHUNK], F32, name="raw%d" % len(chunks), align_bytes=64)
            rows = src[g * K_PASS : (g + 1) * K_PASS, col * CHUNK : (col + PAIR) * CHUNK]
            nc.sync.dma_start(out=piece[:], in_=rows.rearrange("(p j) c -> p j c", j=PACK))
            for i in range(PAIR):
                chunks.append((kind, g, col + i))
                raw.append((piece, i * CHUNK))
        res_sb = {}
        for h in range(T // BANK):
            res_sb[h] = sb.tile([P, TILES, BANK], F32, name="res%d" % h)
            nc.sync.dma_start(out=res_sb[h][:], in_=res[:, h * BANK : (h + 1) * BANK].rearrange("(i p) t -> p i t", p=P))

        eye = sb.tile([P, PACK * K_PASS], BF16, name="eye", align_bytes=64)
        eye_codes = sb.tile([P, K_PASS], U32, name="eye_codes", align_bytes=256)
        eye_scales = sb.tile([P, K_PASS], U8, name="eye_scales", align_bytes=256)
        ramp = sb.tile([P, P * HALF], BF16, name="ramp", align_bytes=64)
        nc.gpsimd.iota(
            ramp[:], pattern=[[1, P * HALF]], base=0, channel_multiplier=-HALF, allow_small_or_imprecise_dtypes=True
        )
        for j in range(PACK):
            nc.vector.tensor_scalar(
                out=eye[:, j * K_PASS : (j + 1) * K_PASS].bitcast(I32),
                in0=ramp[:],
                scalar1=float(j // HALF),
                scalar2=float(BF16_ONE << (16 * (j % HALF))),
                op0=mybir.AluOpType.is_equal,
                op1=mybir.AluOpType.mult,
            )
        for lo in range(0, PACK, HALF):
            nc.vector.quantize_mx(
                out=eye_codes[:, lo * P : (lo + HALF) * P].bitcast(FORMAT["q"]),
                scales=eye_scales[:, lo * P : (lo + HALF) * P],
                in_=eye[:, lo * K_PASS : (lo + HALF) * K_PASS],
            )

        rounded = {}
        codes = {}
        scales = {}
        for kind, cols in (("x", T), ("w", N)):
            for g in range(K // K_PASS):
                for tier in "qr":
                    label = "%s%s%d" % (kind, tier, g)
                    rounded[tier, kind, g] = sb.tile([P, cols * PACK], BF16, name="rounded_" + label, align_bytes=256)
                    codes[tier, kind, g] = sb.tile([P, cols], U32, name="codes_" + label, align_bytes=256)
                    scales[tier, kind, g] = sb.tile([P, cols], U8, name="scales_" + label, align_bytes=256)

        def flat(tier, first, count):
            kind, g, col = chunks[first]
            return rounded[tier, kind, g][:, col * CHUNK * PACK : (col + count) * CHUNK * PACK]

        def interleaved(tier, first, count, run=RUN):
            return flat(tier, first, count).rearrange("p (c i j) -> p c j i", i=run, j=PACK)

        def raw_rows(first, count, run=RUN):
            piece, lo = raw[first]
            return piece[:, :, lo : lo + count * CHUNK].rearrange("p j (c i) -> p c j i", i=run)

        def operand(tier, kind, g, col, count):
            cols = slice(col * CHUNK, (col + count) * CHUNK)
            return codes[tier, kind, g][:, cols].bitcast(FORMAT[tier]), scales[tier, kind, g][:, cols]

        def round_on_scalar(first, count=1):
            nc.scalar.copy(out=interleaved("q", first, count, LINE_RUN), in_=raw_rows(first, count, LINE_RUN))

        def round_on_vector(first):
            nc.vector.tensor_copy(out=interleaved("q", first, 1), in_=raw_rows(first, 1))

        made = []

        def quantise(tier, first, count=1):
            kind, g, col = chunks[first]
            target, plane = operand(tier, kind, g, col, count)
            nc.vector.quantize_mx(out=target, scales=plane, in_=flat(tier, first, count))
            made.extend((tier, kind, g, col + i) for i in range(count))

        back = {}
        words = {}

        def pass_back(target, j, first, count):
            moving, plane = operand("q", *chunks[first], count)
            nc.tensor.matmul_mx(
                out=target,
                lhsT=eye_codes[:, j * P : (j + 1) * P].bitcast(FORMAT["q"]),
                lhsT_scale=eye_scales[:, j * P : (j + 1) * P],
                rhs=moving,
                rhs_scale=plane,
                start=True,
                stop=True,
            )

        def bring_back(first, count=1):
            shape = [P, HALF, PAIR * CHUNK] if first in WIDE else [P, PACK, CHUNK]
            for c in range(first, first + count):
                back[c] = ps.tile(shape, F32, name="back%d" % c, tag="back%d" % (c % BACK_BANKS))
            for j in range(PACK):
                if first in WIDE:
                    pass_back(back[first + j // HALF][:, j % HALF, :], j, first, PAIR)
                else:
                    for c in range(first, first + count):
                        pass_back(back[c][:, j, :], j, c, 1)

        def subtract(c):
            first, u = c - c % PAIR, c % PAIR
            if first not in WIDE:
                target, source = interleaved("r", c, 1), raw_rows(c, 1)
                values = back[c][:].rearrange("p j (c i) -> p c j i", i=RUN)
            else:
                width = HALF * PAIR * CHUNK
                if u == 0:
                    words[first] = sb.tile([P, 2 * width], BF16, name="words%d" % first, align_bytes=64)
                target = words[first][:, u * width : (u + 1) * width].rearrange("p (c i e) -> p c e i", i=HALF_RUN, e=HALF)
                source = raw[first][0][:, HALF * u : HALF * (u + 1), :].rearrange("p e (c i) -> p c e i", i=HALF_RUN)
                values = back[c][:].rearrange("p e (c i) -> p c e i", i=HALF_RUN)
            nc.vector.tensor_tensor(out=target, in0=source, in1=values, op=mybir.AluOpType.subtract)

        def subtract_half(c, half):
            runs = slice(half * CHUNK // (2 * RUN), (half + 1) * CHUNK // (2 * RUN))
            nc.vector.tensor_tensor(
                out=interleaved("r", c, 1)[:, runs],
                in0=raw_rows(c, 1)[:, runs],
                in1=back[c][:].rearrange("p j (c i) -> p c j i", i=RUN)[:, runs],
                op=mybir.AluOpType.subtract,
            )

        def join_words(first):
            nc.scalar.copy(
                out=flat("r", first, PAIR).bitcast(U32).rearrange("p (c i u) -> p c u i", i=RUN, u=2),
                in_=words[first][:].bitcast(U32).rearrange("p (u c i) -> p c u i", i=RUN, u=2),
            )

        acc = {}
        left = [PRODUCTS * count for i, col, count, bank in PARTS]
        parked = {}

        def multiply(part, g, tiers, pair=None):
            i, col, count, bank = PARTS[part]
            lo, count = (0, count) if pair is None else (pair * PAIR, PAIR)
            for w_tier, x_tier in tiers.split():
                opens = part not in acc
                if opens:
                    acc[part] = ps.tile([P, PARTS[part][2] * CHUNK], F32, name="acc_part%d" % part, tag=bank)
                left[part] = left[part] - count
                assert (w_tier, "w", g, i) in made and (x_tier, "x", g, col + lo + count - 1) in made
                stationary, stationary_plane = operand(w_tier, "w", g, i, 1)
                moving, moving_plane = operand(x_tier, "x", g, col + lo, count)
                nc.tensor.matmul_mx(
                    out=acc[part][:, lo * CHUNK : (lo + count) * CHUNK],
                    lhsT=stationary,
                    lhsT_scale=stationary_plane,
                    rhs=moving,
                    rhs_scale=moving_plane,
                    start=opens,
                    stop=left[part] == 0,
                )

        def park(part):
            assert left[part] == 0
            parked[part] = sb.tile([P, BANK], F32, name="parked%d" % part)
            nc.scalar.copy(out=parked[part][:], in_=acc[part][:])

        def add_and_store(part):
            assert left[part] == 0
            i, col, count, bank = PARTS[part]
            lo, width = (col % SLAB) * CHUNK, count * CHUNK
            result = sb.tile([P, width], F32, name="result%d" % part)
            nc.vector.tensor_tensor(
                out=result[:],
                in0=res_sb[col // SLAB][:, i, lo : lo + width],
                in1=parked[part][:] if part in parked else acc[part][:],
                op=mybir.AluOpType.add,
            )
            nc.sync.dma_start(out=out[i * P : (i + 1) * P, col * CHUNK : col * CHUNK + width], in_=result[:])

        round_on_vector(X_A)
        round_on_scalar(X_A + 1)
        for c in (X_A, X_A + 1):
            quantise("q", c)
            bring_back(c)
        round_on_scalar(W_A + 1)
        round_on_vector(W_A)
        quantise("q", W_A)
        bring_back(W_A)
        multiply(0, 0, "qq", pair=0)
        for c in range(X_B, X_K1):
            round_on_scalar(c)
        for first in range(X_K1, X_T0, PAIR):
            round_on_scalar(first, PAIR)
        subtract(X_A)
        quantise("q", W_A + 1)
        bring_back(W_A + 1)
        multiply(1, 0, "qq", pair=0)
        subtract(X_A + 1)
        quantise("r", X_A)
        quantise("q", X_B)
        bring_back(X_B)
        quantise("r", X_A + 1)
        for i in (1, 0):
            multiply(i, 0, "qr", pair=0)
        subtract_half(W_A, 0)
        quantise("q", X_B + 1)
        bring_back(X_B + 1)
        for i in (0, 1):
            multiply(i, 0, "qq", pair=1)
        subtract_half(W_A, 1)
        subtract_half(W_A + 1, 0)
        quantise("q", W_B)
        bring_back(W_B)
        multiply(2, 0, "qq")
        multiply(2, 0, "qr", pair=0)
        subtract_half(W_A + 1, 1)
        quantise("r", W_A)
        quantise("q", W_B + 1)
        quantise("r", W_A + 1)
        multiply(0, 0, "rq")
        multiply(0, 0, "rr", pair=0)
        bring_back(W_B + 1)
        multiply(3, 0, "qq")
        multiply(3, 0, "qr", pair=0)
        multiply(1, 0, "rq")
        multiply(1, 0, "rr", pair=0)
        subtract(X_B)
        subtract(X_B + 1)
        quantise("q", X_K1, PAIR)
        quantise("r", X_B, PAIR)
        bring_back(X_K1, PAIR)
        for i in range(TILES):
            multiply(i, 0, "qr rr" if i < PAIR else "qr", pair=1)
        subtract(W_B)
        quantise("q", X_K1 + PAIR, PAIR)
        bring_back(X_K1 + PAIR)
        subtract(W_B + 1)
        quantise("r", W_B)
        bring_back(X_K1 + PAIR + 1)
        multiply(2, 0, "rq rr")

        subtract(X_K1)
        quantise("r", W_B + 1)
        quantise("q", W_K1, PAIR)
        multiply(3, 0, "rq rr")
        for i in (0, 1):
            multiply(i, 1, "qq")
        subtract(X_K1 + 1)
        join_words(X_K1)
        quantise("q", W_K1 + PAIR, PAIR)
        round_on_scalar(X_T0, PAIR)
        bring_back(W_K1, PAIR)
        for i in (2, 3):
            multiply(i, 1, "qq")
        subtract(X_K1 + 2)
        subtract(X_K1 + 3)
        for first in (X_K1, X_K1 + PAIR):
            quantise("r", first, PAIR)
        for first in range(X_T0 + PAIR, len(chunks), PAIR):
            round_on_scalar(first, PAIR)
        bring_back(W_K1 + PAIR, PAIR)
        for i in (3, 0, 1, 2):
            multiply(i, 1, "qr")
        subtract(W_K1)
        quantise("q", X_T0, PAIR)
        for i in range(TILES):
            subtract(W_K1 + i + 1)
            quantise("r", W_K1 + i)
            if i % PAIR == 0:
                bring_back(X_T0 + i, PAIR)
            else:
                quantise("q", X_T0 + i + 1, PAIR)
            multiply(i, 1, "rq rr")
            if i < PAIR:
                park(i)

        subtract(X_T0 + 1)
        join_words(X_T0)
        bring_back(X_T1, PAIR)
        subtract(X_T0 + 2)
        park(2)
        subtract(X_T0 + 3)
        join_words(X_T0 + PAIR)
        quantise("q", X_T1 + PAIR, PAIR)
        for i in (0, 1):
            multiply(SECOND + i, 0, "qq rq")
        bring_back(X_T1 + PAIR, PAIR)
        multiply(SECOND, 1, "qq rq")
        quantise("r", X_T0, PAIR)
        subtract(X_T1)
        subtract(X_T1 + 1)
        join_words(X_T1)
        quantise("r", X_T0 + PAIR, PAIR)
        multiply(SECOND + 1, 1, "qq rq")
        multiply(SECOND + 2, 0, "qq qr rq rr")
        for i in (0, 1):
            multiply(SECOND + i, 0, "qr rr")
        subtract(X_T1 + 2)
        subtract(X_T1 + 3)
        join_words(X_T1 + PAIR)
        add_and_store(0)
        multiply(SECOND + 2, 1, "qq rq")
        multiply(QUARTER_A, 0, "qq qr rq rr")
        quantise("r", X_T1, PAIR)
        add_and_store(1)
        quantise("r", X_T1 + PAIR, PAIR)

        multiply(SECOND, 1, "qr rr")
        for part in (2, 3, SECOND):
            add_and_store(part)
        for part in (SECOND + 1, SECOND + 2):
            multiply(part, 1, "qr rr")
            add_and_store(part)
        for part in (LAST_HALF, QUARTER_A, QUARTER_B):
            for g in range(1 if part == QUARTER_A else 0, K // K_PASS):
                multiply(part, g, "qq qr rq rr")
            add_and_store(part)
        assert not any(left)
